import numpy as np, ml_dtypes
CORES = [25,29,65,69,153,157,193,197]
N = 8
BF = ml_dtypes.bfloat16
def gentries(a):
    return np.ascontiguousarray(a.reshape(8, 16, -1).transpose(0, 2, 1)).reshape(8, -1)
def gtable(e):
    e = np.asarray(e); return np.ascontiguousarray(e.reshape(8, -1, 16).transpose(0, 2, 1)).reshape(128, -1).astype(np.int32)
B, L, S, RO, ST = 1792, 192, 48, 2, 2
W = B + RO * S
def nodes(rng):
    v = 15 * rng.random((N, 8, 1, B)) + 8 * rng.random((N, 8, 1, B)) * rng.standard_normal((N, 8, 16, B), dtype=np.float32)
    return np.clip(np.rint(v), 0, 15).astype(np.int64)
def kids(rng, share):
    k = rng.integers(1, B, (N, 8, 16, B)); p = (rng.random((N, 8, 1, B)) < share) * rng.random((N, 8, 1, B))
    return np.where(rng.random(k.shape) < p, 0, k)
def ways(rng):
    j = rng.integers(1, B, (N, 8, RO, L - S)); pool = rng.integers(1, B, (N, 8, 48))
    e = np.take_along_axis(pool, rng.integers(0, 48, (N, 8, RO * L)), 2).reshape(N, 8, RO, L)
    return j, np.where(rng.random(e.shape) < 0.4, e, rng.integers(1, B, e.shape))
def far(rng, x, k, j, e):
    for q in range(N):
        for g in range(8):
            o = 1 + rng.permutation(B - 1)[:72]; a, w, v, z = o[:4], o[4:8], o[8:12], o[12:].reshape(4, 15)
            X, K = x[q, g], k[q, g]
            X[:, o] = 0; X[:, w] = 15; X[:, v] = 7; X[:, v[3]] = 15; X[rng.integers(0, 16), v[3]] = 14
            for i in (1, 2): X[:rng.integers(1, 16), z[i, 14]] = 1
            K[:, a[0]] = np.append(w[0], z[0])
            K[:, a[1]] = np.append(z[1], w[1])
            K[:, a[2]] = np.append(z[2], z[2, 0])
            K[:, a[3]] = np.concatenate([v[3:], z[3, :7], w[3:], z[3, 7:14]])
            j[q, g, 0, :4] = np.array([v[0], v[1], w[2], v[3]]); e[q, g, 0, :4] = a
            if rng.random() < 0.5: X[:, o] = 15 - X[:, o]
def pack(x, k, j, e):
    x = np.array(x); k = np.array(k); x[..., 0] = 0; k[..., 0] = 0
    return {"x": np.ascontiguousarray(x.reshape(N, 128, B)).astype(np.float32).astype(BF), "ch": np.ascontiguousarray(k.reshape(N, 128, B)).astype(np.int32),
            "jo": np.stack([gtable(a.reshape(8, -1)) for a in j]), "en": np.stack([gtable(a.reshape(8, -1)) for a in e])}
def setup_inputs(rng):
    share = rng.choice(np.array([0.05, 0.2, 0.4, 0.6]), (N, 8, 1, 1)); j, e = ways(rng)
    return pack(nodes(rng), kids(rng, share), j, e)
def setup_inputs_room(rng):
    x = nodes(rng); k = kids(rng, 0.3); j, e = ways(rng); h = (B - 1) // 2; m = L - S
    for q in range(N):
        for g in range(8):
            o = 1 + rng.permutation(B - 1); full, bare = o[:h], o[h:]
            k[q, g][:, full] = rng.choice(full, (16, h)); k[q, g][:, bare] = 0
            n = int(rng.choice(np.array([0, 1, S - 1, S, S + 1, m])))
            if q == 0: n = (S, S + 1, m, S - 1, 1, 0, S, S + 1)[g]
            stuck = rng.permutation(m) < n
            j[q, g, 0] = np.where(stuck, rng.choice(full, m), rng.choice(bare, m))
            e[q, g, 0, :m] = np.where(stuck, rng.choice(full, m), rng.permutation(bare)[:m])
    return pack(x, k, j, e)
def setup_inputs_ties(rng):
    a = rng.integers(0, 15, (N, 8, 16, 1)); x = a + rng.integers(0, 2, (N, 8, 16, B))
    x[:, 0:4:2] = a[:, 0:4:2] + rng.integers(0, 2, (N, 2, 1, B)); x[:, 3] = a[:, 3]; x[:, 4:] = nodes(rng)[:, 4:]
    j, e = ways(rng); k = kids(rng, 0.1)
    k[:, 1] = rng.integers(1, B, (N, 16, B)); k[:, 4:] = rng.integers(1, B, (N, 4, 16, B)); k[:, 4::2] = 0
    e[:, 4::2] = 1 + np.argsort(rng.random((N, 2, RO, B - 1)), axis=-1)[..., :L]
    for g, i in ((5, 15), (7, 0)):
        k[:, g, i] = k[:, g, i] * rng.integers(0, 2, (N, B))
    return pack(x, k, j, e)
def setup_inputs_alike(rng):
    share = np.full((N, 8, 1, 1), 0.15); share[:, 1] = 0.0; k = kids(rng, share); j, e = ways(rng)
    pool = rng.integers(1, B, (N, 4, 24)); pool[..., 0] = 1; pool[..., 1] = B - 1
    k[:, ::2] = np.where(k[:, ::2] > 0, np.take_along_axis(pool, rng.integers(0, 24, (N, 4, 16 * B)), 2).reshape(N, 4, 16, B), 0)
    k[:, 4, 0] = np.arange(B)
    e[:, 1] = rng.integers(1, B, (N, 1, 1)); j[:, 2] = e[:, 2, :, :L - S]
    e[:, 5] = rng.choice(np.array([1, B - 1]), (N, RO, L)); j[:, 5] = rng.choice(np.array([1, B - 1]), (N, RO, L - S))
    return pack(nodes(rng), k, j, e)
def setup_inputs_guests(rng):
    x = nodes(rng); k = np.zeros((N, 8, 16, B), np.int64); j, e = ways(rng); h = (B - 1) // 4; m = L - S; p = S // 2; at = np.arange(p + 1)
    for q in range(N):
        for g in range(8):
            o = 1 + rng.permutation(B - 1); kin = [o[i:h:4] for i in range(4)]; low, bare = o[h:2 * h], o[2 * h:]
            r, hub, rest = low[:p + 1], low[p + 1:2 * p + 2], low[2 * p + 2:]
            w = rng.integers(0, 4, m); w[0:S:2] = 0; w[1:S:2] = (np.arange(p) + q + g) % 4
            for i in range(4):
                x[q, g][:, kin[i]] = (8, 10, 12, 6)[i]; k[q, g][:, kin[i]] = rng.choice(kin[i], (16, kin[i].size))
                j[q, g, 0] = np.where(w == i, rng.choice(kin[i], m), j[q, g, 0])
                e[q, g, 0, :m] = np.where(w == i, rng.choice(kin[i], m), e[q, g, 0, :m])
            duel = (at < p - 1) & (at % 8 < 4) & (g % 2 == 0)
            via = duel | (at >= p - 1)
            u = rng.integers(0, 16, h); u[:p + 1][duel] = 0
            x[q, g][:, low] = 0; k[q, g][:, low] = rng.choice(rest, (16, h)); k[q, g][u, low] = 0
            k[q, g][:, hub] = r
            for t in range(1, RO):
                e[q, g, t] = rng.permutation(bare)[:L]
                if g == 7: continue
                if t == 1:
                    e[q, g, t, m:] = np.append(np.repeat(r[:p - 1], 2), r[p - 1:])
                    b = hub[via]; e[q, g, t, :b.size] = b; j[q, g, t, :b.size] = rng.choice(kin[2], b.size)
                else:
                    e[q, g, t, :p + 1] = r; j[q, g, t, :p + 1] = rng.choice(kin[2], p + 1)
                    b = r[duel]; e[q, g, t, p + 1:p + 1 + b.size] = b; j[q, g, t, p + 1:p + 1 + b.size] = rng.choice(kin[3], b.size)
    return pack(x, k, j, e)
def setup_inputs_spread(rng):
    x = np.floor(np.exp2(rng.integers(0, 5, (N, 8, 1, B))) * rng.random((N, 8, 16, B))).astype(np.int64); u = rng.random((N, 8, 1, B))
    x = np.where(u < 0.06, 0, np.where(u > 0.94, 15, x)); j, e = ways(rng)
    k = kids(rng, rng.random((N, 8, 1, 1)) ** 2)
    far(rng, x, k, j, e)
    return pack(x, k, j, e)
def check_inputs(d):
    bad = []; v = np.asarray(d["x"]).astype(np.float32)
    if not (np.min(v) >= 0 and np.max(v) <= 15) or np.any(v != np.floor(v)): bad.append("x whole and from 0 to 15")
    if np.any(v[..., 0] != 0): bad.append("column 0 of x")
    if np.any(d["ch"][..., 0] != 0): bad.append("column 0 of ch")
    for k, lo in (("ch", 0), ("jo", 1), ("en", 1)):
        if np.min(d[k]) < lo or np.max(d[k]) > B - 1: bad.append("range of " + k)
    return bad
def cols(t, n):
    return np.take_along_axis(t, n[:, :, None, :], 3)
def slot(t, i):
    return np.take_along_axis(t, i[:, :, None, :], 2)[:, :, 0]
def reference(x, ch, jo, en):
    xs = np.zeros((N, 8, 16, W), np.int64); xs[..., :B] = x.astype(np.float32).astype(np.int64).reshape(N, 8, 16, B)
    cl = np.zeros((N, 8, 16, W), np.int64); cl[..., :B] = ch.astype(np.int64).reshape(N, 8, 16, B)
    jl = np.stack([gentries(a) for a in jo]).astype(np.int64).reshape(N, 8, RO, L - S)
    el = np.stack([gentries(a) for a in en]).astype(np.int64).reshape(N, 8, RO, L)
    lower = np.tril(np.ones((L, L), bool), -1); guest = np.zeros((N, 8, S), bool); ends = []
    for rnd in range(RO):
        gid = np.zeros(S, np.int64) if rnd == 0 else B + (rnd - 1) * S + np.arange(S)
        c = np.concatenate([jl[:, :, rnd], np.broadcast_to(gid, (N, 8, S))], axis=2)
        n = el[:, :, rnd].copy()
        there = np.concatenate([np.ones((N, 8, L - S), bool), guest], axis=2); live = there.copy()
        for step in range(ST):
            before = (n[:, :, :, None] == n[:, :, None, :]) & live[:, :, None, :] & lower
            act = live & ~np.any(before, axis=3)
            xn = cols(xs, n); xc = cols(xs, c); k = cols(cl, n)
            kx = np.take_along_axis(xs, k.reshape(N, 8, 1, 16 * L), 3).reshape(N, 8, 16, 16, L)
            e = np.where(k == 0, 256, np.add.reduce(np.abs(kx - xn[:, :, :, None, :]), axis=2))
            i = np.argmax(e, axis=2); top = slot(e, i)
            has = top == 256
            put = act & (top > np.add.reduce(np.abs(xc - xn), axis=2)); go = act & ~has
            o = np.where(put & ~has, slot(k, i), c)
            s = np.add.reduce(np.abs(kx - cols(xs, o)[:, :, :, None, :]), axis=2)
            s = np.where(put[:, :, None, :] & (np.arange(16)[:, None] == i[:, :, None, :]), 999, s)
            nxt = slot(k, np.argmin(s, axis=2))
            q, g, l = np.nonzero(put); w = n[q, g, l]
            cl[q, g, i[q, g, l], w] = c[q, g, l]
            xs[q, g, :, w] = ((xc + xn) >> 1)[q, g, :, l]
            c = np.where(go, o, c); n = np.where(go, nxt, n); live = live & ~(act & has)
        place = np.add.accumulate(live.astype(np.int64), axis=2) - 1
        q, g, l = np.nonzero(live & (place < S)); p = place[q, g, l]; to = (q + 1 + rnd) % N
        xs[to, g, :, B + rnd * S + p] = xs[q, g, :, c[q, g, l]]
        guest = np.zeros((N, 8, S), bool); guest[to, g, p] = True
        ends.append(np.where(there, n, 0))
    yl = cols(cl, np.concatenate(ends, axis=2))
    return {"yx": xs.reshape(N, 128, W).astype(np.float32).astype(BF), "yl": yl.reshape(N, 128, RO * L).astype(np.float32)}

@@ -1,0 +1,660 @@
+from concourse.mybir import AluOpType, AxisListType, ActivationFunctionType
+
+ALU = AluOpType
+ACT = ActivationFunctionType
+B, L, S, N = 1792, 192, 48, 8
+TR = 192
+U = 65536.0
+CHUNKS = (((0, 64), (64, 80)), ((0, 96), (96, 96)))
+CFG = {"nve": (4, 4, 4, 4), "nvs": (2, 2, 2, 2), "gv": (0.0, 0.0, 0.0, 0.0), "neng": 8, "naS": 0, "ncS": 0, "eq16": 1,
+       "sub": 0.5, "look": 60.0, "alpha": 60.0,
+       "lat": 100.0, "cyc": 1.0, "pe": 0.5, "g": 1.5, "sc": 3.5, "sfix": 100.0, "load": 5000.0, "hop": 4000.0, "tt": 2}
+DT = {"f": "float32", "b": "bfloat16", "i": "int32", "u": "uint16", "h": "float16"}
+
+
+def col(a, c0, c1, step=1):
+    return (a[0], a[1], a[2], a[3] + c0, a[3] + c1, step)
+
+
+def par(a, p):
+    return (a[0], 0, p, a[3], a[4], a[5])
+
+
+def width(a):
+    if a[0] == "ind":
+        return 16 * width(a[2])
+    return (a[4] - a[3] + a[5] - 1) // a[5]
+
+
+def ind(win, off):
+    return ("ind", win, off)
+
+
+def build(cfg):
+    ops = []
+    top = {"f": 0, "b": 0, "i": 0, "u": 0, "h": 0}
+    cyc, gth, sct = cfg["cyc"], cfg["g"], cfg["sc"]
+
+    def new(k, n):
+        a = top[k]
+        top[k] = a + (n + 15) // 16 * 16
+        return ("a" + k, 0, 128, a, a + n, 1)
+
+    def bank(i, n, p=128):
+        return ("ps%d" % i, 0, p, 0, n, 1)
+
+    def flat(xs):
+        r = []
+        for a in xs:
+            if isinstance(a, tuple):
+                r += [a[1], a[2]] if a[0] == "ind" else [a]
+        return r
+
+    def add(eng, kind, args, out, ins, cost, **kw):
+        rd = flat(ins)
+        wr = [out]
+        if out[0] == "ind":
+            wr = [out[1]]
+            rd = rd + [out[2]]
+        o = {"eng": eng, "kind": kind, "args": args, "rd": rd, "wr": wr, "cost": cost, "n": len(ops), "after": []}
+        o.update(kw)
+        ops.append(o)
+        return o
+
+    def two(a):
+        return a[0] in ("ab", "au", "ah", "xt", "sb0", "sb1")
+
+    def vcost(out, ins, rate):
+        n = width(out)
+        if out[0] == "ind":
+            return 50 + sct * n * cyc
+        if ins[0][0] == "ind":
+            return 50 + gth * n * cyc
+        return 15 + max(64, rate * n) * cyc
+
+    def cp(out, a):
+        return add("V", "cp", (out, a), out, [a], vcost(out, [a], 0.5 if two(out) and two(a) else 1))
+
+    def tt(out, a, b, op):
+        r = 1 if a[0][:2] == "ps" or b[0][:2] == "ps" else cfg["tt"]
+        return add("V", "tt", (out, a, b, op), out, [a, b], vcost(out, [a], r))
+
+    def ts(out, a, s1, op0, s2=None, op1=None):
+        return add("V", "ts", (out, a, s1, s2, op0, op1), out, [a, s1, s2], vcost(out, [a], 0.5 if two(out) and two(a) else 1))
+
+    def ms(out, v):
+        return add("V", "ms", (out, v), out, [], vcost(out, [out], 0.5 if two(out) else 1))
+
+    def scan(out, d0, d1, init, op0, op1):
+        return add("V", "scan", (out, d0, d1, init, op0, op1), out, [d0, d1], vcost(out, [d0], 1))
+
+    def act(out, a, f, bias=0.0, scale=1.0):
+        c = 65 + gth * width(out) * cyc if a[0] == "ind" else cfg["sfix"] + width(out) * cyc
+        return add("S", "act", (out, a, f, bias, scale), out, [a], c)
+
+    def mm(out, lhs, rhs, grp=None):
+        c = max(min(64, width(lhs)), width(rhs)) * cfg["pe"] * (4 if lhs[0] == "af" else 1)
+        o = add("P", "mm", (out, lhs, rhs), out, [lhs, rhs], c, grp=grp)
+        if grp is not None:
+            grp.append(o)
+        return o
+
+    def iota(out, pat, base=0, cm=0):
+        return add("G", "iota", (out, pat, base, cm), out, [], 130 + 2 * width(out) * cyc)
+
+    def dma(eng, out, a, dur, sem):
+        return add(eng, "dma", (out, a), out, [a], 60.0, dur=dur, sem=sem)
+
+    XT = ("xt", 0, 128, 0, 2048, 1)
+    CT = ("ct", 0, 128, 0, 2032, 1)
+    dr = lambda nm, a, b: (nm, 0, 128, a, b, 1)
+
+    eni, joi = new("i", 24), new("i", 18)
+    dma("Y", eni, dr("en", 0, 24), 2000.0, "ld0")
+    dma("Y", col(CT, TR, TR + B), dr("ch", 0, B), cfg["load"], "ld1")
+    dma("S", joi, dr("jo", 0, 18), 2000.0, "ld2")
+    dma("S", col(XT, TR, TR + B), dr("x", 0, B), cfg["load"], "ld3")
+
+    pi, t_i = new("i", 1), new("i", 2)
+    idt = new("f", B + S)
+    JB, JR, G18, PJ = new("f", 128), new("f", 128), new("f", 144), new("f", 144)
+    s18i, s4i = new("i", 144), new("i", 144)
+    iota(pi, [[0, 1]], 0, 1)
+    iota(col(idt, 0, 256), [[1, 256]])
+    iota(JB, [[1, 8], [0, 16]])
+    iota(PJ, [[32, 8], [1, 18]])
+    iota(G18, [[1, 8], [0, 18]])
+    iota(s18i, [[0, 8], [1, 18]])
+    iota(JR, [[0, 8], [1, 16]])
+    iota(col(CT, TR + B, TR + B + S), [[0, S]])
+    for a, b in ((256, 512), (512, 1024), (1024, B + S)):
+        act(col(idt, a, b), col(idt, 0, b - a), ACT.Identity, float(a))
+
+    def fill(out, v):
+        return act(out, col(idt, 0, width(out)), ACT.Identity, v, 0.0)
+
+    def scale(out, a, v):
+        return act(out, a, ACT.Identity, 0.0, v)
+
+    cols = new("f", 8)
+    pc, gcol, rc, sf, cA, cN, pw, p32 = [col(cols, j, j + 1) for j in range(8)]
+    cp(pc, pi)
+    ts(col(t_i, 0, 1), pi, 4, ALU.arith_shift_right)
+    ts(col(t_i, 1, 2), pi, 15, ALU.bitwise_and)
+    cp(col(cols, 1, 3), t_i)
+    ts(p32, gcol, 16.0, ALU.mult, pc, ALU.add)
+    I, NI, I4, BO, TRI, ONE, t1 = [new("b", 128) for _ in range(7)]
+    IH, M16 = new("h", 128), new("f", 128)
+    ts(I, col(idt, 0, 128), pc, ALU.is_equal)
+    scale(NI, I, -1.0)
+    scale(I4, I, 4096.0)
+    cp(IH, I)
+    ts(BO, JB, gcol, ALU.is_equal)
+    ts(M16, JR, rc, ALU.is_equal)
+    fill(ONE, 1.0)
+    add("G", "sel", (t1, BO, [[1, 128]], ALU.is_gt, 0.0, 0, -1), t1, [BO], 170 + 256 * cyc)
+    add("G", "sel", (TRI, t1, [[1, 128]], ALU.not_equal, -4096.0, 0, -1), TRI, [t1], 170 + 256 * cyc)
+    B8f = new("f", 8)
+    B8 = {}
+    ts(B8f, col(idt, 0, 8), gcol, ALU.is_equal)
+    for v in (1, -1, 2, -2):
+        B8[v] = new("b", 8)
+        scale(B8[v], B8f, v * U)
+    ga, PAY, P0 = new("b", 144), new("h", 144), new("h", 144)
+    ts(ga, G18, gcol, ALU.is_equal)
+    ts(PAY, PJ, p32, ALU.is_equal)
+    NEm, CI, NA8 = new("b", 144), new("b", 144), new("b", 8)
+    ts(NEm, PAY, -256 * U, ALU.mult)
+    ts(sf, rc, -2048.0, ALU.mult, 15 * 2048.0, ALU.add)
+    ts(CI, PAY, sf, ALU.mult)
+    tA = new("f", 1)
+    ts(tA, rc, 0.0, ALU.is_equal, 32768.0, ALU.mult)
+    ts(cA, tA, -32 * 32768.0, ALU.add)
+    ts(cN, tA, -15.0, ALU.mult, 96 * 32768.0, ALU.add)
+    ts(col(CI, 16, 144, 18), B8f, cA, ALU.mult)
+    ts(col(CI, 17, 144, 18), B8f, -2.0 ** 21, ALU.mult)
+    ts(NA8, B8f, cN, ALU.mult)
+    XV = {}
+    ts(s4i, s18i, 19, ALU.bitwise_and)
+    if cfg["ncS"]:
+        P8, IF = new("f", 8), new("f", 128)
+        scale(P8, B8f, -1.0 / 16)
+        scale(IF, I, 1.0)
+    else:
+        tw = new("b", 144)
+        ts(tw, s4i, 16.0, ALU.is_ge, -1.0 / 16, ALU.mult)
+        tt(P0, ga, tw, ALU.mult)
+    for sg, nv in sorted(set((-1, v) for v in cfg["nve"]) | set((1, v) for v in cfg["nvs"])):
+        tv = new("b", 144)
+        ts(tv, s4i, float(nv), ALU.is_lt, sg * U, ALU.mult)
+        XV[sg, nv] = new("b", 144)
+        tt(XV[sg, nv], ga, tv, ALU.mult)
+    R18 = new("f", 144)
+    fill(R18, 0.0)
+    ms(col(R18, 0, 144, 18), -2.0 ** 26)
+    xoff = new("u", 8)
+    ts(xoff, col(idt, 0, 8), 18.0, ALU.mult, 17.0, ALU.add)
+    lanew, lm, tr2 = new("f", 12), new("f", 12), new("f", 12)
+    ts(lanew, col(idt, 0, L, 16), rc, ALU.add)
+    act(lm, lanew, ACT.Identity, -float(TR))
+    act(tr2, lanew, ACT.Identity, float(L - 4096))
+    half, PW = new("b", L), new("f", L)
+    thr = new("b", L)
+    E, c128 = new("b", 32), new("b", L)
+    ms(half, 0.5)
+    ms(c128, -128.0)
+    scan(PW, half, c128, 2.0 ** 96, ALU.mult, ALU.max)
+    scale(thr, PW, -2.5 / 128 if cfg["naS"] else 2.5)
+    tp, tq, wc = new("f", 16), new("f", 1), new("f", 12)
+    tt(tp, col(PW, 0, 16), col(M16, 0, 16), ALU.mult)
+    add("V", "red", (tq, tp), tq, [tp], 80.0)
+    ts(pw, tq, 2.0 ** -95, ALU.mult)
+    ts(wc, col(PW, 0, L, 16), pw, ALU.mult)
+    ts(E, col(idt, 0, 32), rc, ALU.add, 15.0, ALU.is_equal)
+    SB = [("sb%d" % t, 0, 128, 0, 2 * L, 1) for t in range(2)]
+    for t in range(2):
+        fill(col(SB[t], 0, 64), 0.0)
+    SC = [new("f", 144) for _ in range(2)]
+    for q in range(2):
+        fill(SC[q], 0.0)
+    nend = new("u", 24)
+    ms(col(nend, 9, 12), 0)
+
+    KX = [new("b", 16 * L) for _ in range(2)]
+    EL = [[new("b", 16 * 96) for _ in range(2)] for _ in range(2)]
+    EQ = [new("b", 1248) for _ in range(2)]
+    AX = [new("f", 128) for _ in range(2)]
+    KB, XB, DB, M0, M1 = (0, 1), (2, 3), (4, 5), 6, 7
+    dnext = [0]
+    LB = ("lb", 0, 128, 0, S, 1)
+
+    def distances(q, m, kx, xr, sg, nv, key, grp, el, cut=0):
+        last = []
+        xp = bank(XB[q], 4 * m)
+        for j in range(4):
+            mm(col(xp, j, 4 * m, 4), I, xr)
+        ox = mm(key, xr, XV[-sg, nv], grp)
+        for c in (0, 3, 1, 2):
+            e = col(el, c * 4 * m, (c + 1) * 4 * m)
+            if c < nv:
+                for a, b in ((0, cut), (cut, m)):
+                    if b > a:
+                        tt(col(e, 4 * a, 4 * b), col(kx, 16 * a + c, 16 * b, 4), col(xp, 4 * a, 4 * b), ALU.max)
+            else:
+                d = bank(DB[dnext[0] % 2], 4 * m)
+                dnext[0] += 1
+                dg = []
+                mm(d, I, col(kx, c, 16 * m, 4), dg)
+                for j in range(4):
+                    mm(col(d, j, 4 * m, 4), NI, xr, dg)
+                act(e, d, ACT.Abs)
+            for j in range(4):
+                s = c + 4 * j
+                if c < nv:
+                    ok = mm(col(key, s, 144, 18), col(kx, s, 16 * m, 16), B8[-sg], grp)
+                o = mm(col(key, s, 144, 18), col(e, j, 4 * m, 4), B8[2 * sg if c < nv else sg], grp)
+                if c < nv:
+                    o["after"] += [ox, ok]
+                    last.append(o)
+        return last
+
+    def pick(q, m, key, ovr, wi):
+        scan(par(SC[q], m), par(R18, m), key, 0.0, ALU.add, ALU.max)
+        tt(AX[q], ind(SC[q], xoff), M16, ALU.mult)
+        w = bank(XB[q], m // 16)
+        mm(w, par(AX[q], m), par(col(B8f, 0, m // 16), m))
+        if ovr is None:
+            cp(wi, w)
+        else:
+            tt(wi, w, ovr, ALU.max)
+
+    st = {}
+    for rnd in range(2):
+        Lr = L - S if rnd == 0 else L
+        nb = Lr // 16
+        NW = B if rnd == 0 else B + S
+        al = lambda a: col(a, 0, nb)
+        nu, nf, cu = new("u", 12), new("f", 12), new("u", 12)
+        cp(al(nu), col(eni, 12 * rnd, 12 * rnd + nb))
+        cp(al(nf), col(eni, 12 * rnd, 12 * rnd + nb))
+        cp(col(cu, 0, 9), col(joi, 9 * rnd, 9 * rnd + 9))
+        live = None
+        if rnd == 1:
+            ts(col(cu, 9, 12), col(lanew, 0, 3), float(B), ALU.add)
+            live = new("f", 12)
+            ms(col(live, 0, 9), 1.0)
+            ts(col(live, 9, 12), col(lanew, 0, 3), col(XT, TR + B + S, TR + B + S + 1), ALU.is_lt)
+        for step in range(2):
+            si = 2 * rnd + step
+            guests = si == 2
+            nw1 = B if step == 0 else NW
+            xw1, xw = col(XT, TR, TR + nw1), col(XT, TR, TR + NW)
+            ku, kf, ncr = new("u", Lr), new("h", Lr), new("f" if cfg["ncS"] else "h", Lr)
+            nrep = new("u" if cfg["eq16"] else "f", Lr)
+            xn, xc, xo, ne, ad, bl, na, mask = [new("b", Lr) for _ in range(8)]
+            wi, oi, qi, sj, ni, nj, zi = [new("i", 12) for _ in range(7)]
+            ou, su, wu = new("u", 12), new("u", 12), new("u", 12)
+            wl, ovr, nB, hh, sov, nz, a1, a2 = [new("f", 12) for _ in range(8)]
+            nu2 = new("u", 12) if step == 0 else col(nend, 12 * rnd, 12 * rnd + 12)
+            nf2 = new("f", 12)
+            live2 = new("f" if step == 0 else "b", 12)
+            kxs = KX[si % 2]
+            ch = [(q, l0, m, l0 // 16, (l0 + m) // 16) for q, (l0, m) in enumerate(CHUNKS[rnd])]
+            for q, l0, m, b0, b1 in ch:
+                ln = lambda a: col(a, l0, l0 + m)
+                wr = lambda a: col(a, b0, b1)
+                cp(ln(ku), ind(col(CT, TR, TR + nw1), wr(nu)))
+                act(ln(xn), ind(xw1, wr(nu)), ACT.Identity, -7.5)
+                mv = int(round(m * cfg["gv"][si] / 2)) * 2
+                cut = max(mv, int(m * cfg["sub"]) // 2 * 2)
+                for a, b, eng in ((0, mv, "V"), (mv, cut, "S"), (cut, m, "S")):
+                    if b > a:
+                        o_, i_ = col(kxs, 16 * (l0 + a), 16 * (l0 + b)), ind(xw1, col(ku, l0 + a, l0 + b))
+                        if eng == "S":
+                            act(o_, i_, ACT.Identity, -7.5)
+                        else:
+                            ts(o_, i_, -7.5, ALU.add)
+            cp(kf, ku)
+            ts(ne, ku, 0.0, ALU.is_gt)
+            if cfg["ncS"]:
+                act(ncr, ind(idt, al(cu)), ACT.Identity, 0.0, -1.0)
+            else:
+                ts(ncr, ind(idt, al(cu)), -1.0, ALU.mult)
+            if guests:
+                act(col(xc, 0, L - S), ind(xw1, col(cu, 0, 9)), ACT.Identity, -7.5)
+                act(col(xc, L - S, L), col(XT, TR + B, TR + B + S), ACT.Identity, -7.5)
+            else:
+                act(xc, ind(xw, al(cu)), ACT.Identity, -7.5)
+            if cfg["eq16"]:
+                cp(nrep, ind(idt, al(nu)))
+            else:
+                act(nrep, ind(idt, al(nu)), ACT.Identity)
+            if live is not None:
+                f0 = 6 if guests else 0
+                tt(col(wl, f0, nb), col(live, f0, nb), col(wc, f0, nb), ALU.mult)
+                ts(col(ovr, f0, nb), col(live, f0, nb), -2.0 ** 25 - (512 * U + 32768), ALU.mult, 512 * U + 32768, ALU.add)
+            eq, at = [], 0
+            for b in range(nb):
+                e = col(EQ[si % 2], at - 16 * b, at - 16 * b + Lr)
+                at += Lr - 16 * b
+                wq = wc if live is None or (guests and b < 9) else wl
+                ts(col(e, 16 * b, Lr), col(nrep, 16 * b, Lr), col(nf, b, b + 1), ALU.is_equal, col(wq, b, b + 1), ALU.mult)
+                eq.append(e)
+            for l0, m in (CHUNKS[1] if guests else ((0, Lr),)):
+                ln = lambda a: col(a, l0, l0 + m)
+                pm = bank(M0, 2 * m)
+                g1, g2, g3 = [], [], []
+                mm(col(pm, 0, m), I, ln(xc), g1)
+                mm(col(pm, 0, m), NI, ln(xn), g1)
+                mm(col(pm, m, 2 * m), I, ln(xc), g2)
+                mm(col(pm, m, 2 * m), I, ln(xn), g2)
+                act(ln(ad), col(pm, 0, m), ACT.Abs)
+                act(ln(bl), col(pm, m, 2 * m), ACT.Identity, 135.25, 0.5)
+                cn = bank(M1, m)
+                if cfg["naS"]:
+                    mm(cn, ONE, ln(thr), g3)
+                for b in range((l0 + m) // 16):
+                    c0 = max(l0, 16 * b)
+                    mm(col(cn, c0 - l0, m), BO, col(eq[b], c0, l0 + m), g3)
+                if cfg["naS"]:
+                    act(ln(na), cn, ACT.Sign)
+                else:
+                    tt(ln(na), cn, ln(thr), ALU.is_ge)
+            for q, l0, m, b0, b1 in ch:
+                ln = lambda a: col(a, l0, l0 + m)
+                wr = lambda a: col(a, b0, b1)
+                key, grp = bank(KB[q], 144, m), []
+                kx = col(kxs, 16 * l0, 16 * (l0 + m))
+                mm(key, col(ONE, 0, m), CI, grp)
+                mm(key, ln(kf), PAY, grp)
+                mm(col(key, 16, 144, 18), ln(ad), B8[1], grp)
+                o = mm(col(key, 17, 144, 18), ln(na), NA8, grp)
+                if cfg["ncS"]:
+                    mm(col(key, 16, 144, 18), ln(ncr), P8, grp)
+                    mm(col(key, 17, 144, 18), ln(ncr), P8, grp)["after"].append(o)
+                else:
+                    mm(key, ln(ncr), P0, grp)["after"].append(o)
+                last = distances(q, m, kx, ln(xn), 1, cfg["nve"][si], key, grp, EL[q][0], int(m * cfg["sub"]) // 2 * 2)
+                mm(key, ln(ne), NEm, grp)["after"].extend(last)
+                pick(q, m, key, None if live is None or (guests and q == 0) else wr(ovr), wr(wi))
+                ts(wr(oi), wr(wi), 2047, ALU.bitwise_and)
+                cp(wr(ou), wr(oi))
+                act(ln(xo), ind(xw, wr(ou)), ACT.Identity, -7.5)
+            ts(al(sj), al(wi), 11, ALU.arith_shift_right, 31, ALU.bitwise_and)
+            cp(al(su), al(sj))
+            act(mask, ind(E, al(su)), ACT.Identity)
+            if guests:
+                tt(al(nz), al(nf), al(live), ALU.mult)
+            ts(al(nB), al(nz if guests else nf), U, ALU.add)
+            ts(al(hh), al(wi), U, ALU.add, 32.0, ALU.mult)
+            tt(al(sov), al(hh), al(nB), ALU.min)
+            ts(al(qi), al(wi), 32768, ALU.bitwise_and)
+            tt(al(a1), al(nf), al(qi), ALU.subtract)
+            tt(al(a2), al(a1), al(lm), ALU.max)
+            ts(al(wu), al(a2), float(TR), ALU.add)
+            tt(ind(col(XT, 0, TR + NW), al(wu)), bl, col(c128, 0, Lr), ALU.add)
+            ts(al(zi), al(wi), 19, ALU.arith_shift_right, 63, ALU.bitwise_and)
+            ts(al(live2), al(zi), 31.0, ALU.is_ge)
+            if step == 1:
+                inc, xs_, b1_, pu = new("b", 12), new("b", Lr), new("f", 12), new("u", 12)
+                scan(al(inc), col(ONE, 0, nb), al(live2), 0.0, ALU.mult, ALU.add)
+                pp, gp = bank(M1, 16), []
+                mm(col(pp, 0, nb), TRI, al(live2), gp)
+                mm(col(pp, 1, nb), BO, col(inc, 0, nb - 1), gp)
+                if rnd == 0:
+                    mm(col(pp, 12, 13), BO, col(inc, nb - 1, nb))
+                tt(al(b1_), col(pp, 0, nb), al(tr2), ALU.min)
+                ts(al(pu), al(b1_), 4096.0, ALU.add)
+                act(xs_, ind(xw, al(ou)), ACT.Identity)
+                cp(ind(SB[rnd], al(pu)), xs_)
+                if rnd == 0:
+                    cp(col(SB[0], S, S + 1), col(pp, 12, 13))
+                w = 64 if rnd == 0 else S
+                tok = ("tok%d" % rnd, 0, 128, 0, 1, 1)
+                st["send%d" % rnd] = add("G", "send", (rnd, col(SB[rnd], 0, w)), tok, [col(SB[rnd], 0, w)], 300.0,
+                                         dur=1500.0, sem="snt%d" % rnd)
+            pa, pb, ga_, gb_ = bank(M1, Lr), bank(M0, Lr), [], []
+            bb, nl = new("f", Lr), new("i", Lr)
+            mm(pb, IF if cfg["ncS"] else IH, ncr, gb_)
+            mm(pb, I4, mask, gb_)
+            mm(pa, IH, kf, ga_)
+            mm(pa, I4, mask, ga_)
+            act(bb, pb, ACT.Identity, 4096.0, -1.0)
+            tt(nl, pa, bb, ALU.min)
+            cp(ind(col(CT, 0, TR + NW), al(wu)), nl)
+            for q, l0, m, b0, b1 in ch:
+                ln = lambda a: col(a, l0, l0 + m)
+                wr = lambda a: col(a, b0, b1)
+                key, grp = bank(KB[q], 144, m), []
+                kx = col(kxs, 16 * l0, 16 * (l0 + m))
+                mm(key, col(ONE, 0, m), CI, grp)
+                mm(key, ln(kf), PAY, grp)
+                distances(q, m, kx, ln(xo), -1, cfg["nvs"][si], key, grp, EL[q][1])
+                mm(key, ln(mask), NEm, grp)
+                pick(q, m, key, wr(sov), wr(ni))
+                ts(wr(nj), wr(ni), 2047, ALU.bitwise_and)
+                cp(wr(nu2), wr(nj))
+            if step == 0:
+                cp(al(nf2), al(nj))
+            else:
+                land = col(XT, TR + B, TR + B + 64) if rnd == 0 else LB
+                o = add("X", "arrive", (rnd,), land, [], 0.0, dur=cfg["hop"], sem="arr%d" % rnd)
+                o["soft"] = st["send%d" % rnd]
+            nu, nf, cu, live = nu2, nf2, ou, live2
+    yf = new("f", 2 * L)
+    cw = col(CT, TR, TR + B + S)
+    o = dma("Y", dr("yx", 0, B + S), col(XT, TR, TR + B + S), 3000.0, "st0")
+    o["after"].append(st["send1"])
+    dma("Y", dr("yx", B + S, B + 2 * S), LB, 2000.0, "st1")
+    for t in range(2):
+        cp(col(yf, t * L, t * L + L), ind(cw, col(nend, 12 * t, 12 * t + 12)))
+        dma("S", dr("yl", t * L, t * L + L), col(yf, t * L, t * L + L), 2000.0, "st%d" % (2 + t))
+    return ops, top
+
+
+def link(ops):
+    seen = {}
+    for o in ops:
+        deps, order = set(), set()
+        acc = [(a, False) for a in o["rd"]] + [(a, True) for a in o["wr"]]
+        for a, w in acc:
+            ps = a[0][:2] == "ps"
+            for (p, b, pw) in seen.get(a[0], ()):
+                if ps and p["eng"] != o["eng"]:
+                    deps.add(p["n"])
+                elif ps and o["eng"] == "P":
+                    if o["grp"] is None or p["grp"] is not o["grp"] or o["grp"][0] is p:
+                        order.add(p["n"])
+                elif (w or pw) and a[3] < b[4] and b[3] < a[4]:
+                    deps.add(p["n"])
+        for a, w in acc:
+            seen.setdefault(a[0], []).append((o, a, w))
+        for p in o["after"]:
+            (order if p["eng"] == "P" and o["eng"] == "P" else deps).add(p["n"])
+        if o["kind"] == "arrive":
+            deps = set()
+        o["deps"], o["order"] = deps, order - deps
+
+
+def schedule(ops, cfg):
+    lat = cfg["lat"]
+    n = len(ops)
+    pre = [[(d, lat) for d in o["deps"]] + [(d, 0.0) for d in o["order"]] for o in ops]
+    for o in ops:
+        if "soft" in o:
+            pre[o["n"]].append((o["soft"]["n"], 0.0))
+    suc = [[] for _ in ops]
+    for i in range(n):
+        for d, l in pre[i]:
+            suc[d].append((i, l))
+    span = [o["cost"] + o.get("dur", 0.0) for o in ops]
+    prio = [0.0] * n
+    for i in range(n - 1, -1, -1):
+        prio[i] = span[i] + max([prio[j] + l for j, l in suc[i]] + [0.0])
+    left = [len(p) for p in pre]
+    rdy = [0.0] * n
+    free = {}
+    queues = {}
+    pool = [i for i in range(n) if left[i] == 0]
+    end = 0.0
+    while pool:
+        t0, e0 = min((max(rdy[i], free.get(ops[i]["eng"], 0.0)), ops[i]["eng"]) for i in pool)
+        cand = [i for i in pool if ops[i]["eng"] == e0 and rdy[i] <= t0 + cfg["look"]]
+        i = max(cand, key=lambda j: (prio[j] - cfg["alpha"] * max(0.0, rdy[j] - t0), -j))
+        pool.remove(i)
+        o = ops[i]
+        s = max(t0, rdy[i])
+        o["t"] = s
+        free[e0] = s + o["cost"]
+        queues.setdefault(e0, []).append(o)
+        fin = s + span[i]
+        end = max(end, fin)
+        for j, l in suc[i]:
+            rdy[j] = max(rdy[j], fin + l)
+            left[j] -= 1
+            if left[j] == 0:
+                pool.append(j)
+    return queues, end
+
+
+def plan(cfg):
+    ops, top = build(cfg)
+    link(ops)
+    queues, end = schedule(ops, cfg)
+    pos = {}
+    for e, qu in queues.items():
+        for k, o in enumerate(qu):
+            pos[o["n"]] = k
+    for e, qu in queues.items():
+        got = {}
+        for o in qu:
+            need = {}
+            for d in o["deps"]:
+                p = ops[d]
+                k = p.get("sem") or p["eng"]
+                if pos[d] > got.get(k, -1) and pos[d] > need.get(k, (-1, None))[0]:
+                    need[k] = (pos[d], p)
+            o["waits"] = [v[1] for v in need.values()]
+            for k, v in need.items():
+                got[k] = v[0]
+                v[1]["sig"] = True
+    total = {}
+    for e, qu in queues.items():
+        c = 0
+        for o in qu:
+            if "sem" not in o and o.get("sig"):
+                c += 1
+                o["cnt"] = c
+        total[e] = c
+    for o in queues["P"]:
+        gr = o["grp"]
+        o["start"] = gr is None or gr[0] is o
+        o["stop"] = gr is None or max(pos[p["n"]] for p in gr) == pos[o["n"]]
+    return ops, top, queues, total, end
+
+
+PLAN = plan(CFG)
+SCRATCH = {"xt": ("sbuf", [128, 2048], "bfloat16"), "ct": ("sbuf", [128, 2032], "int32"),
+           "sb0": ("sbuf", [128, 2 * L], "bfloat16"), "sb1": ("sbuf", [128, 2 * L], "bfloat16"),
+           "lb": ("dram", [128, S], "bfloat16"),
+           "rb0": ("sbuf", [128, 64], "bfloat16"), "rb1": ("dram", [128, S], "bfloat16")}
+for _k in "fbiuh":
+    SCRATCH["a" + _k] = ("sbuf", [128, PLAN[1][_k]], DT[_k])
+for _k in range(8):
+    SCRATCH["ps%d" % _k] = ("psum", [128, 512], "float32")
+SEMAPHORES = ["cV", "cS", "cP", "cG", "ld0", "ld1", "ld2", "ld3", "st0", "st1", "st2", "st3",
+              "snt0", "snt1", "arr0", "arr1", "rin0", "rin1", "rout"]
+
+
+def relay_of(core, cores, topo):
+    r = cores.index(core)
+    dsts = [cores[(r + 1 + t) % N] for t in range(2)]
+    ok = [c for c in topo.cores_of(core) if c not in cores and all(topo.may_write(c, d) for d in dsts)]
+    near = [c for c in ok if topo.die(c) == topo.die(core)]
+    return near[0]
+
+
+def some(engines, k):
+    m = 0
+    for e in engines[:k]:
+        m |= 1 << e
+    return m
+
+
+def rank_program(g, core, T, topo):
+    cores = list(T.cores)
+    ne = CFG["neng"]
+    ops, top, queues, total, end = PLAN
+
+    def ap(a):
+        if not isinstance(a, tuple):
+            return a
+        if a[0] == "ind":
+            return ap(a[1]).indirect(ap(a[2]))
+        if a[5] == 1:
+            return T[a[0]][a[1]:a[2], a[3]:a[4]]
+        return T[a[0]][a[1]:a[2], a[3]:a[4]:a[5]]
+
+    rank = T.rank_of(core)
+    if rank is None:
+        for r, c in enumerate(cores):
+            if relay_of(c, cores, topo) == core:
+                far = cores[(r + 2) % N]
+                for t in range(2):
+                    d = cores[(r + 1 + t) % N]
+                    rid, pid = topo.addr(d, core)
+                    eng = [e for e in topo.engines(core, d) if e in topo.engines(core, far)]
+                    land = T.xt[:, TR + B:TR + B + 64] if t == 0 else T.lb[:]
+                    g.wait_ge(T.sem["rin%d" % t], ne)
+                    g.remote_dma(land, T["rb%d" % t][:], T.sem["arr%d" % t], T.sem.rout, pid, rid, some(eng, ne))
+                g.wait_ge(T.sem.rout, 2 * ne)
+        return
+
+    relay = relay_of(core, cores, topo)
+    eng = {"V": g.vector, "S": g.scalar, "P": g.tensor, "G": g, "Y": g.sync}
+    for e in ("Y", "S", "G", "V", "P"):
+        q = eng[e]
+        for o in queues[e]:
+            for p in o["waits"]:
+                if "sem" in p:
+                    q.wait_ge(T.sem[p["sem"]], 16 if p["kind"] == "dma" else ne)
+                else:
+                    q.wait_ge(T.sem["c" + p["eng"]], p["cnt"])
+            k = o["kind"]
+            a = [ap(v) for v in o["args"]]
+            if k == "send":
+                t = o["args"][0]
+                rid, pid = topo.addr(relay, core)
+                g.remote_dma(T["rb%d" % t][:], a[1], T.sem["rin%d" % t], T.sem["snt%d" % t], pid, rid,
+                             some(topo.engines(core, relay)[::-1], ne))
+                continue
+            if k == "dma":
+                q.dma_start(a[0], a[1]).then_inc(T.sem[o["sem"]], 16)
+                continue
+            if k == "cp":
+                r = q.tensor_copy(a[0], a[1])
+            elif k == "tt":
+                r = q.tensor_tensor(a[0], a[1], a[2], a[3])
+            elif k == "ts":
+                r = q.tensor_scalar(a[0], a[1], a[2], a[3], a[4]) if a[5] is None else q.tensor_scalar(*a)
+            elif k == "ms":
+                r = q.memset(a[0], a[1])
+            elif k == "scan":
+                r = q.tensor_tensor_scan(*a)
+            elif k == "red":
+                r = q.tensor_reduce(a[0], a[1], AxisListType.X, ALU.add)
+            elif k == "act":
+                r = q.activation(a[0], a[1], a[2], bias=a[3], scale=a[4])
+            elif k == "mm":
+                r = q.matmul(a[0], a[1], a[2], o["start"], o["stop"])
+            elif k == "sel":
+                r = q.affine_select(*a)
+            elif o["args"][0][0] in ("ai", "ct"):
+                r = q.iota(a[0], a[1], a[2], a[3])
+            else:
+                r = q.iota(a[0], a[1], a[2], a[3], allow_small_or_imprecise_dtypes=True)
+            if o.get("sig"):
+                r.then_inc(T.sem["c" + e], 1)
+    g.wait_ge(T.sem.snt0, ne)
+    for s in ("st0", "st1", "st2", "st3"):
+        g.wait_ge(T.sem[s], 16)

@@ -3,12 +3,18 @@ from concourse.mybir import AluOpType, AxisListType, ActivationFunctionType
 ALU = AluOpType
 ACT = ActivationFunctionType
 B, L, S, N = 1792, 192, 48, 8
-TR = 192
+TR = 2 * L
 U = 65536.0
-CHUNKS = (((0, 64), (64, 80)), ((0, 96), (96, 96)))
-CFG = {"nve": (4, 4, 4, 4), "nvs": (2, 2, 2, 2), "gv": (0.0, 0.0, 0.0, 0.0), "neng": 8, "naS": 0, "ncS": 0, "eq16": 1,
-       "sub": 0.5, "look": 60.0, "alpha": 60.0,
-       "lat": 100.0, "cyc": 1.0, "pe": 0.5, "g": 1.5, "sc": 3.5, "sfix": 100.0, "load": 5000.0, "hop": 4000.0, "tt": 2}
+WAIT = 505 * U
+BIG = 2.0 ** 26
+CLS = (0, 4, 2, 6, 1, 5, 3, 7)
+CFG = {"blocks": (((0, 64), (64, 80)), ((0, 96), (96, 96))),
+       "nve": ((8, 8), (8, 8), (6, 8), (8, 8)), "nvs": ((8, 8), (6, 6), (6, 6), (6, 2)),
+       "gv": ((0.67, 0.0), (0.33, 0.5), (0.25, 0.25), (0.0, 0.25)), "sub": (0.5, 0.5, 0, 0.5),
+       "cS": (1, 0, 1, 1), "late": (0, 1), "mg": (1, 1, 1, 1), "neng": 8,
+       "bx": (0, 2, 2, 0), "tS": (0, 0, 0, 0), "share": 0, "rep": (4, 4), "xf": 1, "one": (6, 4, 7, 4),
+       "look": 400.0, "alpha": 60.0, "lat": 170.0, "lats": 210.0, "latp": 30.0, "latS": 60.0, "cyc": 0.83, "pe": 0.33,
+       "g": 1.3, "sc": 2.8, "vfix": 12.0, "mn": 25, "vr": 0.7, "sfix": 200.0, "ldc": 3400.0, "ldx": 3700.0, "hop": 3000.0}
 DT = {"f": "float32", "b": "bfloat16", "i": "int32", "u": "uint16", "h": "float16"}
 
 
@@ -30,10 +36,27 @@ def ind(win, off):
     return ("ind", win, off)
 
 
+def cost(o, cfg):
+    kind, n = o["shape"]
+    cyc = cfg["cyc"]
+    if kind == "fix":
+        return n
+    if kind == "pe":
+        return cfg.get("pfix", 0) + n * cfg["pe"]
+    if kind == "g":
+        return 130 + 2 * n * cyc
+    if kind == "gather":
+        return (50 if o["eng"] == "V" else 65) + cfg["g"] * n * cyc
+    if kind == "scatter":
+        return 50 + cfg["sc"] * n * cyc
+    if o["kind"] == "tt" and "ps" in (o["args"][1][0][:2], o["args"][2][0][:2]):
+        n = n * cfg.get("vr", 1)
+    return cfg["vfix" if o["eng"] == "V" else "sfix"] + max(cfg.get("mn", 64), n) * cyc
+
+
 def build(cfg):
     ops = []
     top = {"f": 0, "b": 0, "i": 0, "u": 0, "h": 0}
-    cyc, gth, sct = cfg["cyc"], cfg["g"], cfg["sc"]
 
     def new(k, n):
         a = top[k]
@@ -50,13 +73,13 @@ def build(cfg):
                 r += [a[1], a[2]] if a[0] == "ind" else [a]
         return r
 
-    def add(eng, kind, args, out, ins, cost, **kw):
+    def add(eng, kind, args, out, ins, shape, **kw):
         rd = flat(ins)
         wr = [out]
         if out[0] == "ind":
             wr = [out[1]]
             rd = rd + [out[2]]
-        o = {"eng": eng, "kind": kind, "args": args, "rd": rd, "wr": wr, "cost": cost, "n": len(ops), "after": []}
+        o = {"eng": eng, "kind": kind, "args": args, "rd": rd, "wr": wr, "shape": shape, "n": len(ops), "after": []}
         o.update(kw)
         ops.append(o)
         return o
@@ -64,390 +87,480 @@ def build(cfg):
     def two(a):
         return a[0] in ("ab", "au", "ah", "xt", "sb0", "sb1")
 
-    def vcost(out, ins, rate):
+    def shape(out, a, rate):
         n = width(out)
         if out[0] == "ind":
-            return 50 + sct * n * cyc
-        if ins[0][0] == "ind":
-            return 50 + gth * n * cyc
-        return 15 + max(64, rate * n) * cyc
+            return ("scatter", n)
+        if a[0] == "ind":
+            return ("gather", n)
+        return ("flat", rate * n)
 
     def cp(out, a):
-        return add("V", "cp", (out, a), out, [a], vcost(out, [a], 0.5 if two(out) and two(a) else 1))
+        return add("V", "cp", (out, a), out, [a], shape(out, a, 0.5 if two(out) and two(a) else 1))
 
     def tt(out, a, b, op):
-        r = 1 if a[0][:2] == "ps" or b[0][:2] == "ps" else cfg["tt"]
-        return add("V", "tt", (out, a, b, op), out, [a, b], vcost(out, [a], r))
+        return add("V", "tt", (out, a, b, op), out, [a, b], shape(out, a, 1 if a[0][:2] == "ps" or b[0][:2] == "ps" else 2))
 
     def ts(out, a, s1, op0, s2=None, op1=None):
-        return add("V", "ts", (out, a, s1, s2, op0, op1), out, [a, s1, s2], vcost(out, [a], 0.5 if two(out) and two(a) else 1))
+        return add("V", "ts", (out, a, s1, s2, op0, op1), out, [a, s1, s2], shape(out, a, 0.5 if two(out) and two(a) else 1))
 
     def ms(out, v):
-        return add("V", "ms", (out, v), out, [], vcost(out, [out], 0.5 if two(out) else 1))
+        return add("V", "ms", (out, v), out, [], shape(out, out, 0.5 if two(out) else 1))
 
     def scan(out, d0, d1, init, op0, op1):
-        return add("V", "scan", (out, d0, d1, init, op0, op1), out, [d0, d1], vcost(out, [d0], 1))
+        return add("V", "scan", (out, d0, d1, init, op0, op1), out, [d0, d1], shape(out, d0, 1))
 
-    def act(out, a, f, bias=0.0, scale=1.0):
-        c = 65 + gth * width(out) * cyc if a[0] == "ind" else cfg["sfix"] + width(out) * cyc
-        return add("S", "act", (out, a, f, bias, scale), out, [a], c)
+    def act(out, a, f=ACT.Identity, bias=0.0, scale=1.0):
+        return add("S", "act", (out, a, f, bias, scale), out, [a], shape(out, a, 1))
 
     def mm(out, lhs, rhs, grp=None):
-        c = max(min(64, width(lhs)), width(rhs)) * cfg["pe"] * (4 if lhs[0] == "af" else 1)
-        o = add("P", "mm", (out, lhs, rhs), out, [lhs, rhs], c, grp=grp)
+        c = max(min(64, width(lhs)), width(rhs)) * (4 if lhs[0] == "af" else 1)
+        o = add("P", "mm", (out, lhs, rhs), out, [lhs, rhs], ("pe", c), grp=grp)
         if grp is not None:
             grp.append(o)
         return o
 
     def iota(out, pat, base=0, cm=0):
-        return add("G", "iota", (out, pat, base, cm), out, [], 130 + 2 * width(out) * cyc)
+        return add("G", "iota", (out, pat, base, cm), out, [], ("g", width(out)))
 
     def dma(eng, out, a, dur, sem):
-        return add(eng, "dma", (out, a), out, [a], 60.0, dur=dur, sem=sem)
+        return add(eng, "dma", (out, a), out, [a], ("fix", 60.0), dur=dur, sem=sem)
 
-    XT = ("xt", 0, 128, 0, 2048, 1)
-    CT = ("ct", 0, 128, 0, 2032, 1)
+    XT = ("xt", 0, 128, 0, TR + B + 64, 1)
+    CT = ("ct", 0, 128, 0, TR + B + S, 1)
     dr = lambda nm, a, b: (nm, 0, 128, a, b, 1)
 
     eni, joi = new("i", 24), new("i", 18)
-    dma("Y", eni, dr("en", 0, 24), 2000.0, "ld0")
-    dma("Y", col(CT, TR, TR + B), dr("ch", 0, B), cfg["load"], "ld1")
-    dma("S", joi, dr("jo", 0, 18), 2000.0, "ld2")
-    dma("S", col(XT, TR, TR + B), dr("x", 0, B), cfg["load"], "ld3")
+    if cfg["xf"] == 2:
+        dma("Y", eni, dr("en", 0, 24), 2000.0, "ld0")
+        dma("Y", col(CT, TR, TR + B), dr("ch", 0, B), cfg["ldc"], "ld1")
+        dma("S", joi, dr("jo", 0, 18), 2000.0, "ld2")
+        dma("S", col(XT, TR, TR + B), dr("x", 0, B), cfg["ldx"], "ld3")
+        ms(col(XT, TR, TR + 1), 31.0)
+    elif cfg["xf"]:
+        dma("S", eni, dr("en", 0, 24), 2000.0, "ld0")
+        dma("S", joi, dr("jo", 0, 18), 2000.0, "ld2")
+        o = dma("Y", col(XT, TR, TR + B), dr("x", 0, B), 1500 + (cfg["ldx"] - 1500) / 3, "ld3")
+        dma("Y", col(CT, TR, TR + B), dr("ch", 0, B), cfg["ldx"], "ld1")["behind"] = o
+        ms(col(XT, TR, TR + 1), 31.0)
+    else:
+        ms(col(XT, TR, TR + 1), 31.0)
+        dma("Y", eni, dr("en", 0, 24), 2000.0, "ld0")
+        dma("Y", col(CT, TR, TR + B), dr("ch", 0, B), cfg["ldc"], "ld1")
+        dma("S", joi, dr("jo", 0, 18), 2000.0, "ld2")
+        dma("S", col(XT, TR + 1, TR + B), dr("x", 1, B), cfg["ldx"], "ld3")["after"].append(ops[0])
 
     pi, t_i = new("i", 1), new("i", 2)
-    idt = new("f", B + S)
-    JB, JR, G18, PJ = new("f", 128), new("f", 128), new("f", 144), new("f", 144)
-    s18i, s4i = new("i", 144), new("i", 144)
+    idt, ids = new("f", 256), new("f", TR + B + S)
+    JB, JR = new("f", 128), new("f", L)
     iota(pi, [[0, 1]], 0, 1)
-    iota(col(idt, 0, 256), [[1, 256]])
+    iota(idt, [[1, 256]])
     iota(JB, [[1, 8], [0, 16]])
-    iota(PJ, [[32, 8], [1, 18]])
-    iota(G18, [[1, 8], [0, 18]])
-    iota(s18i, [[0, 8], [1, 18]])
-    iota(JR, [[0, 8], [1, 16]])
+    iota(JR, [[0, 12], [1, 16]])
+    iota(col(CT, 0, TR), [[0, TR]])
     iota(col(CT, TR + B, TR + B + S), [[0, S]])
-    for a, b in ((256, 512), (512, 1024), (1024, B + S)):
-        act(col(idt, a, b), col(idt, 0, b - a), ACT.Identity, float(a))
-
-    def fill(out, v):
-        return act(out, col(idt, 0, width(out)), ACT.Identity, v, 0.0)
-
-    def scale(out, a, v):
-        return act(out, a, ACT.Identity, 0.0, v)
+    ms(col(XT, 0, TR), 0.0)
+    act(col(ids, 0, 256), idt, ACT.Identity, -4096.0)
+    if cfg["xf"]:
+        ts(col(ids, 256, 512), idt, 256 - 4096.0, ALU.add)
+        for a, b, on_s in ((512, 1024, 1), (1024, 1536, 0), (1536, 2048, 1), (2048, TR + B + S, 0)):
+            if on_s:
+                act(col(ids, a, b), col(ids, 0, b - a), ACT.Identity, float(a))
+            else:
+                ts(col(ids, a, b), col(ids, 0, b - a), float(a), ALU.add)
+    else:
+        for a, b in ((256, 512), (512, 1024), (1024, 2048), (2048, TR + B + S)):
+            act(col(ids, a, b), col(ids, 0, b - a), ACT.Identity, float(a))
 
     cols = new("f", 8)
-    pc, gcol, rc, sf, cA, cN, pw, p32 = [col(cols, j, j + 1) for j in range(8)]
+    pc, gcol, rc, sfE, sfS, r31 = [col(cols, j, j + 1) for j in range(6)]
     cp(pc, pi)
     ts(col(t_i, 0, 1), pi, 4, ALU.arith_shift_right)
     ts(col(t_i, 1, 2), pi, 15, ALU.bitwise_and)
     cp(col(cols, 1, 3), t_i)
-    ts(p32, gcol, 16.0, ALU.mult, pc, ALU.add)
-    I, NI, I4, BO, TRI, ONE, t1 = [new("b", 128) for _ in range(7)]
-    IH, M16 = new("h", 128), new("f", 128)
+    ts(r31, rc, -1.0, ALU.mult, 31.0, ALU.add)
+    I, NI, I8, BO, NBO, TRI, t1 = [new("b", 128) for _ in range(7)]
+    IH2 = new("h", 256)
+    IH = col(IH2, 0, 128)
+    M16, R16, OFF = new("f", L), new("f", L), new("b", L)
     ts(I, col(idt, 0, 128), pc, ALU.is_equal)
-    scale(NI, I, -1.0)
-    scale(I4, I, 4096.0)
+    act(NI, I, ACT.Identity, 0.0, -1.0)
+    act(I8, I, ACT.Identity, 0.0, -8192.0)
     cp(IH, I)
-    ts(BO, JB, gcol, ALU.is_equal)
+    cp(col(IH2, 128, 256), I)
+    ts(BO, JB, gcol, ALU.is_equal, U, ALU.mult)
+    act(NBO, BO, ACT.Identity, 0.0, -1.0)
     ts(M16, JR, rc, ALU.is_equal)
-    fill(ONE, 1.0)
-    add("G", "sel", (t1, BO, [[1, 128]], ALU.is_gt, 0.0, 0, -1), t1, [BO], 170 + 256 * cyc)
-    add("G", "sel", (TRI, t1, [[1, 128]], ALU.not_equal, -4096.0, 0, -1), TRI, [t1], 170 + 256 * cyc)
-    B8f = new("f", 8)
+    act(OFF, M16, ACT.Identity, -2.0 ** 36, 5 * 2.0 ** 34)
+    add("G", "sel", (t1, BO, [[1, 128]], ALU.is_gt, 0.0, 0, -1), t1, [BO], ("g", 148))
+    add("G", "sel", (TRI, t1, [[1, 128]], ALU.not_equal, -512 * U, 0, -1), TRI, [t1], ("g", 148))
+    B8f, RH, BK = new("f", 8), new("f", 8), new("b", 32)
     B8 = {}
     ts(B8f, col(idt, 0, 8), gcol, ALU.is_equal)
-    for v in (1, -1, 2, -2):
-        B8[v] = new("b", 8)
-        scale(B8[v], B8f, v * U)
-    ga, PAY, P0 = new("b", 144), new("h", 144), new("h", 144)
-    ts(ga, G18, gcol, ALU.is_equal)
-    ts(PAY, PJ, p32, ALU.is_equal)
-    NEm, CI, NA8 = new("b", 144), new("b", 144), new("b", 8)
-    ts(NEm, PAY, -256 * U, ALU.mult)
-    ts(sf, rc, -2048.0, ALU.mult, 15 * 2048.0, ALU.add)
-    ts(CI, PAY, sf, ALU.mult)
-    tA = new("f", 1)
-    ts(tA, rc, 0.0, ALU.is_equal, 32768.0, ALU.mult)
-    ts(cA, tA, -32 * 32768.0, ALU.add)
-    ts(cN, tA, -15.0, ALU.mult, 96 * 32768.0, ALU.add)
-    ts(col(CI, 16, 144, 18), B8f, cA, ALU.mult)
-    ts(col(CI, 17, 144, 18), B8f, -2.0 ** 21, ALU.mult)
-    ts(NA8, B8f, cN, ALU.mult)
-    XV = {}
-    ts(s4i, s18i, 19, ALU.bitwise_and)
-    if cfg["ncS"]:
-        P8, IF = new("f", 8), new("f", 128)
-        scale(P8, B8f, -1.0 / 16)
-        scale(IF, I, 1.0)
-    else:
-        tw = new("b", 144)
-        ts(tw, s4i, 16.0, ALU.is_ge, -1.0 / 16, ALU.mult)
-        tt(P0, ga, tw, ALU.mult)
-    for sg, nv in sorted(set((-1, v) for v in cfg["nve"]) | set((1, v) for v in cfg["nvs"])):
-        tv = new("b", 144)
-        ts(tv, s4i, float(nv), ALU.is_lt, sg * U, ALU.mult)
-        XV[sg, nv] = new("b", 144)
-        tt(XV[sg, nv], ga, tv, ALU.mult)
-    R18 = new("f", 144)
-    fill(R18, 0.0)
-    ms(col(R18, 0, 144, 18), -2.0 ** 26)
+    ts(RH, B8f, col(B8f, 7, 8), ALU.add)
+    for k, v in enumerate((1, -1, 2, -2)):
+        B8[v] = col(BK, 8 * k, 8 * k + 8)
+        ts(B8[v], B8f, v * U, ALU.mult)
+    if 1 in cfg["cS"]:
+        IF = new("f", 128)
+        act(IF, I)
+    act(R16, JR, ACT.Identity, 0.0, 0.0)
+    ms(col(R16, 0, L, 16), -2.0 ** 40)
+    RK = [new("f", 128) for _ in range(2)]
+    act(RK[0], col(R16, 0, 128), ACT.Identity, 2048.0)
+    act(RK[1], col(R16, 0, 128), ACT.Identity, 4096.0)
     xoff = new("u", 8)
-    ts(xoff, col(idt, 0, 8), 18.0, ALU.mult, 17.0, ALU.add)
-    lanew, lm, tr2 = new("f", 12), new("f", 12), new("f", 12)
+    ts(xoff, col(idt, 0, 8), 16.0, ALU.mult, 15.0, ALU.add)
+    lanew, blank, tr2 = new("f", 12), new("f", 12), new("f", 12)
     ts(lanew, col(idt, 0, L, 16), rc, ALU.add)
-    act(lm, lanew, ACT.Identity, -float(TR))
-    act(tr2, lanew, ACT.Identity, float(L - 4096))
-    half, PW = new("b", L), new("f", L)
-    thr = new("b", L)
-    E, c128 = new("b", 32), new("b", L)
-    ms(half, 0.5)
-    ms(c128, -128.0)
-    scan(PW, half, c128, 2.0 ** 96, ALU.mult, ALU.max)
-    scale(thr, PW, -2.5 / 128 if cfg["naS"] else 2.5)
-    tp, tq, wc = new("f", 16), new("f", 1), new("f", 12)
-    tt(tp, col(PW, 0, 16), col(M16, 0, 16), ALU.mult)
-    add("V", "red", (tq, tp), tq, [tp], 80.0)
-    ts(pw, tq, 2.0 ** -95, ALU.mult)
-    ts(wc, col(PW, 0, L, 16), pw, ALU.mult)
-    ts(E, col(idt, 0, 32), rc, ALU.add, 15.0, ALU.is_equal)
+    ts(blank, lanew, float(L), ALU.add)
+    ts(tr2, lanew, L - 512.0, ALU.add, U, ALU.mult)
+    E, c160, ONE = new("b", 32), new("b", L), new("b", 12)
+    ts(E, col(idt, 0, 32), r31, ALU.is_equal, 4096.0, ALU.mult)
+    if 0 in cfg["bx"]:
+        act(c160, JR, ACT.Identity, -160.0, 0.0)
+    ms(ONE, 1.0)
     SB = [("sb%d" % t, 0, 128, 0, 2 * L, 1) for t in range(2)]
     for t in range(2):
-        fill(col(SB[t], 0, 64), 0.0)
-    SC = [new("f", 144) for _ in range(2)]
-    for q in range(2):
-        fill(SC[q], 0.0)
+        act(col(SB[t], 0, 64), col(idt, 0, 64), ACT.Identity, 0.0, 0.0)
+    SC = []
+    for v in (16 * 2048 - 256 * U, TR - U):
+        sc = new("f", 256)
+        act(sc, idt, ACT.Identity, v, 0.0)
+        SC.append([col(sc, 0, 128), col(sc, 128, 256)])
     nend = new("u", 24)
-    ms(col(nend, 9, 12), 0)
+    ms(col(nend, 8, 12), TR)
 
-    KX = [new("b", 16 * L) for _ in range(2)]
-    EL = [[new("b", 16 * 96) for _ in range(2)] for _ in range(2)]
+    KX = [new("b", 16 * L) for _ in range(3)]
+    EL = [[new("b", 16 * 112) for _ in range(2)] for _ in range(2)]
     EQ = [new("b", 1248) for _ in range(2)]
     AX = [new("f", 128) for _ in range(2)]
     KB, XB, DB, M0, M1 = (0, 1), (2, 3), (4, 5), 6, 7
     dnext = [0]
     LB = ("lb", 0, 128, 0, S, 1)
 
-    def distances(q, m, kx, xr, sg, nv, key, grp, el, cut=0):
-        last = []
-        xp = bank(XB[q], 4 * m)
-        for j in range(4):
-            mm(col(xp, j, 4 * m, 4), I, xr)
-        ox = mm(key, xr, XV[-sg, nv], grp)
-        for c in (0, 3, 1, 2):
-            e = col(el, c * 4 * m, (c + 1) * 4 * m)
-            if c < nv:
-                for a, b in ((0, cut), (cut, m)):
-                    if b > a:
-                        tt(col(e, 4 * a, 4 * b), col(kx, 16 * a + c, 16 * b, 4), col(xp, 4 * a, 4 * b), ALU.max)
-            else:
-                d = bank(DB[dnext[0] % 2], 4 * m)
+    def open_keys(q, m, kx, kfq, nvs):
+        keys, grp = bank(KB[q], 256, m), []
+        lo, hi = min(nvs), max(nvs) + 1
+        mm(col(keys, 128 * lo, 128 * hi), kfq, col(IH2, 128 * lo, 128 * hi), grp)
+        sums = []
+        for s in range(16):
+            use = [k for k in nvs if s % 8 in CLS[:nvs[k]]]
+            if use:
+                a, b = use[0], use[-1] + 1
+                sums.append(mm(col(keys, 128 * a + s, 128 * b, 16), col(kx, s, 16 * m, 16), col(BK, 8 * a, 8 * b), grp))
+        return keys, grp, sums
+
+    def distances(q, m, kx, xr, sg, nv, key, grp, sums, el, rep, cut=0):
+        def units(cs, r):
+            us = []
+            for c in cs:
+                if r == 4 and c >= 4 and c - 4 in cs:
+                    continue
+                us += [(c, 4)] if r == 4 and c + 4 in cs else [(c, 8)] if r > 1 else [(c, 16), (c + 8, 16)]
+            return us
+        vs, ss = units(CLS[:nv], rep), units(CLS[nv:], 4)
+        xps, at = {}, 0
+        for r in sorted(set(16 // st for c, st in vs)):
+            xps[r] = col(bank(XB[q], 512), at, at + r * m)
+            at += r * m
+            for j in range(r):
+                mm(col(xps[r], j, r * m, r), I, xr)
+        mins, at = [], 0
+        todo = sorted([(k / len(vs), 0, u) for k, u in enumerate(vs)] + [(k / len(ss), 1, u) for k, u in enumerate(ss)])
+        for _, on_s, (c, st) in todo:
+            r = 16 // st
+            e = col(el, at, at + r * m)
+            at += r * m
+            if on_s:
+                d = bank(DB[dnext[0] % 2], r * m)
                 dnext[0] += 1
                 dg = []
-                mm(d, I, col(kx, c, 16 * m, 4), dg)
-                for j in range(4):
-                    mm(col(d, j, 4 * m, 4), NI, xr, dg)
+                mm(d, I, col(kx, c, 16 * m, st), dg)
+                for j in range(r):
+                    mm(col(d, j, r * m, r), NI, xr, dg)
                 act(e, d, ACT.Abs)
-            for j in range(4):
-                s = c + 4 * j
-                if c < nv:
-                    ok = mm(col(key, s, 144, 18), col(kx, s, 16 * m, 16), B8[-sg], grp)
-                o = mm(col(key, s, 144, 18), col(e, j, 4 * m, 4), B8[2 * sg if c < nv else sg], grp)
-                if c < nv:
-                    o["after"] += [ox, ok]
-                    last.append(o)
-        return last
+            else:
+                for a, b in ((0, cut), (cut, m)):
+                    if b > a:
+                        tt(col(e, r * a, r * b), col(kx, 16 * a + c, 16 * b, st), col(xps[r], r * a, r * b), ALU.min)
+            for j in range(r):
+                o = mm(col(key, c + st * j, 128, 16), col(e, j, r * m, r), B8[sg if on_s else -2 * sg], grp)
+                if not on_s:
+                    o["after"] += sums
+                    mins.append(o)
+        at = 0
+        for n in (8, 4, 2, 1):
+            if nv & n:
+                c = CLS[at]
+                at += n
+                mm(col(key, c, 128, 8 // n), xr, col(BO if sg > 0 else NBO, c, 128, 8 // n), grp)["after"] += mins
 
-    def pick(q, m, key, ovr, wi):
-        scan(par(SC[q], m), par(R18, m), key, 0.0, ALU.add, ALU.max)
-        tt(AX[q], ind(SC[q], xoff), M16, ALU.mult)
+    def pick(k, q, m, key, ovr, wi):
+        scan(par(SC[k][q], m), par(RK[k], m), key, 0.0, ALU.add, ALU.max)
+        tt(AX[q], ind(SC[k][q], xoff), col(M16, 0, 128), ALU.mult)
         w = bank(XB[q], m // 16)
-        mm(w, par(AX[q], m), par(col(B8f, 0, m // 16), m))
-        if ovr is None:
-            cp(wi, w)
-        else:
-            tt(wi, w, ovr, ALU.max)
+        mm(w, AX[q], col(RH, 0, m // 16))
+        tt(wi, w, ovr, ALU.max)
 
+    def lower(pd, gp, nu, nf, nb, buf):
+        Lr, at = 16 * nb, 0
+        nrep = new("u", Lr)
+        ts(nrep, ind(ids, col(nu, 0, nb)), 4096.0, ALU.add)
+        mm(pd, I, col(OFF, 0, Lr), gp)
+        for b in range(nb):
+            e = col(buf, at, at + Lr - 16 * b)
+            at += Lr - 16 * b
+            ts(e, col(nrep, 16 * b, Lr), col(nf, b, b + 1), ALU.is_equal, 512.0, ALU.mult)
+            mm(col(pd, 16 * b, 16 * b + 16), TRI, col(e, 0, 16), gp)
+            if b + 1 < nb:
+                mm(col(pd, 16 * b + 16, Lr), BO, col(e, 16, Lr - 16 * b), gp)
+
+    nu0, nf0, off2 = new("u", 24), new("f", 24), new("b", L)
+    ts(nu0, eni, float(TR), ALU.add)
+    ts(nf0, eni, float(TR), ALU.add)
+    lower(bank(DB[1], L), [], col(nu0, 12, 24), col(nf0, 12, 24), 12, EQ[1])
+    act(off2, bank(DB[1], L))
+    cu0, cB0 = new("u", 24), new("f", 24)
     st = {}
+    late = {}
     for rnd in range(2):
         Lr = L - S if rnd == 0 else L
         nb = Lr // 16
         NW = B if rnd == 0 else B + S
         al = lambda a: col(a, 0, nb)
-        nu, nf, cu = new("u", 12), new("f", 12), new("u", 12)
-        cp(al(nu), col(eni, 12 * rnd, 12 * rnd + nb))
-        cp(al(nf), col(eni, 12 * rnd, 12 * rnd + nb))
+        nu, nf, cu, cB = [col(a, 12 * rnd, 12 * rnd + 12) for a in (nu0, nf0, cu0, cB0)]
         cp(col(cu, 0, 9), col(joi, 9 * rnd, 9 * rnd + 9))
-        live = None
+        ts(col(cB, 0, 9), col(joi, 9 * rnd, 9 * rnd + 9), 250 * U, ALU.add)
+        z0 = nf
         if rnd == 1:
             ts(col(cu, 9, 12), col(lanew, 0, 3), float(B), ALU.add)
-            live = new("f", 12)
-            ms(col(live, 0, 9), 1.0)
-            ts(col(live, 9, 12), col(lanew, 0, 3), col(XT, TR + B + S, TR + B + S + 1), ALU.is_lt)
+            ts(col(cB, 9, 12), col(lanew, 0, 3), B + 250 * U, ALU.add)
+            cnt = col(XT, TR + B + S, TR + B + S + 1)
+            lone, z0, zt = new("f", 3), new("f", 12), new("f", 3)
+            cp(col(z0, 0, 9), col(nf, 0, 9))
+            ts(lone, col(lanew, 0, 3), cnt, ALU.is_lt)
+            tt(zt, col(nf, 9, 12), lone, ALU.mult)
+            ts(col(z0, 9, 12), zt, float(TR), ALU.max)
         for step in range(2):
             si = 2 * rnd + step
             guests = si == 2
             nw1 = B if step == 0 else NW
             xw1, xw = col(XT, TR, TR + nw1), col(XT, TR, TR + NW)
-            ku, kf, ncr = new("u", Lr), new("h", Lr), new("f" if cfg["ncS"] else "h", Lr)
-            nrep = new("u" if cfg["eq16"] else "f", Lr)
-            xn, xc, xo, ne, ad, bl, na, mask = [new("b", Lr) for _ in range(8)]
-            wi, oi, qi, sj, ni, nj, zi = [new("i", 12) for _ in range(7)]
+            ku, kf = new("u", Lr), new("h", Lr)
+            xn, xc, xo, ad, bl, mask = [new("b", Lr) for _ in range(6)]
+            wi, oi, fq, ni, nj = [new("i", 12) for _ in range(5)]
             ou, su, wu = new("u", 12), new("u", 12), new("u", 12)
-            wl, ovr, nB, hh, sov, nz, a1, a2 = [new("f", 12) for _ in range(8)]
+            vm, th, ovr, hh, sov, keep, a1, a2, cB2, nf2 = [new("f", 12) for _ in range(10)]
             nu2 = new("u", 12) if step == 0 else col(nend, 12 * rnd, 12 * rnd + 12)
-            nf2 = new("f", 12)
-            live2 = new("f" if step == 0 else "b", 12)
-            kxs = KX[si % 2]
-            ch = [(q, l0, m, l0 // 16, (l0 + m) // 16) for q, (l0, m) in enumerate(CHUNKS[rnd])]
+            sd, cm, nl = new("f", Lr), new("f", Lr), new("i", Lr)
+            kxs = KX[(0, 1, 0, 2)[si]]
+            ch = [(q, l0, m, l0 // 16, (l0 + m) // 16) for q, (l0, m) in enumerate(cfg["blocks"][rnd])]
+            one = cfg["one"][si]
             for q, l0, m, b0, b1 in ch:
                 ln = lambda a: col(a, l0, l0 + m)
                 wr = lambda a: col(a, b0, b1)
-                cp(ln(ku), ind(col(CT, TR, TR + nw1), wr(nu)))
-                act(ln(xn), ind(xw1, wr(nu)), ACT.Identity, -7.5)
-                mv = int(round(m * cfg["gv"][si] / 2)) * 2
-                cut = max(mv, int(m * cfg["sub"]) // 2 * 2)
-                for a, b, eng in ((0, mv, "V"), (mv, cut, "S"), (cut, m, "S")):
+                if not one & 1:
+                    cp(ln(ku), ind(col(CT, 0, TR + nw1), wr(nu)))
+                elif q == 0:
+                    cp(ku, ind(col(CT, 0, TR + nw1), al(nu)))
+                if not one & 2:
+                    act(ln(xn), ind(col(XT, 0, TR + nw1), wr(nu)))
+                elif q == 0:
+                    act(xn, ind(col(XT, 0, TR + nw1), al(nu)))
+                mv = int(round(m * cfg["gv"][si][q] / 2)) * 2
+                cut = max(mv, int(m * cfg["sub"][si]) // 2 * 2)
+                for a, b, eng in ((0, mv, cp), (mv, cut, act), (cut, m, act)):
                     if b > a:
-                        o_, i_ = col(kxs, 16 * (l0 + a), 16 * (l0 + b)), ind(xw1, col(ku, l0 + a, l0 + b))
-                        if eng == "S":
-                            act(o_, i_, ACT.Identity, -7.5)
-                        else:
-                            ts(o_, i_, -7.5, ALU.add)
-            cp(kf, ku)
-            ts(ne, ku, 0.0, ALU.is_gt)
-            if cfg["ncS"]:
-                act(ncr, ind(idt, al(cu)), ACT.Identity, 0.0, -1.0)
-            else:
-                ts(ncr, ind(idt, al(cu)), -1.0, ALU.mult)
+                        eng(col(kxs, 16 * (l0 + a), 16 * (l0 + b)), ind(xw1, col(ku, l0 + a, l0 + b)))
+                if not one & 4:
+                    cp(ln(kf), ln(ku))
+            if one & 4:
+                cp(kf, ku)
+            if cfg["cS"][si]:
+                crep = new("f", Lr)
+                act(crep, ind(ids, al(cu)))
             if guests:
-                act(col(xc, 0, L - S), ind(xw1, col(cu, 0, 9)), ACT.Identity, -7.5)
-                act(col(xc, L - S, L), col(XT, TR + B, TR + B + S), ACT.Identity, -7.5)
+                act(col(xc, 0, L - S), ind(xw1, col(cu, 0, 9)))
             else:
-                act(xc, ind(xw, al(cu)), ACT.Identity, -7.5)
-            if cfg["eq16"]:
-                cp(nrep, ind(idt, al(nu)))
+                act(xc, ind(xw, al(cu)))
+            if cfg["bx"][si]:
+                x160 = new("b", Lr)
+                if cfg["bx"][si] == 1:
+                    ts(x160, xn, -160.0, ALU.add)
+                else:
+                    act(x160, xn, ACT.Identity, -160.0)
             else:
-                act(nrep, ind(idt, al(nu)), ACT.Identity)
-            if live is not None:
-                f0 = 6 if guests else 0
-                tt(col(wl, f0, nb), col(live, f0, nb), col(wc, f0, nb), ALU.mult)
-                ts(col(ovr, f0, nb), col(live, f0, nb), -2.0 ** 25 - (512 * U + 32768), ALU.mult, 512 * U + 32768, ALU.add)
-            eq, at = [], 0
-            for b in range(nb):
-                e = col(EQ[si % 2], at - 16 * b, at - 16 * b + Lr)
-                at += Lr - 16 * b
-                wq = wc if live is None or (guests and b < 9) else wl
-                ts(col(e, 16 * b, Lr), col(nrep, 16 * b, Lr), col(nf, b, b + 1), ALU.is_equal, col(wq, b, b + 1), ALU.mult)
-                eq.append(e)
-            for l0, m in (CHUNKS[1] if guests else ((0, Lr),)):
+                x160 = col(c160, 0, Lr)
+            both = {}
+
+            def stays(l0, m):
+                b0, b1 = l0 // 16, (l0 + m) // 16
                 ln = lambda a: col(a, l0, l0 + m)
+                wr = lambda a: col(a, b0, b1)
                 pm = bank(M0, 2 * m)
                 g1, g2, g3 = [], [], []
-                mm(col(pm, 0, m), I, ln(xc), g1)
-                mm(col(pm, 0, m), NI, ln(xn), g1)
-                mm(col(pm, m, 2 * m), I, ln(xc), g2)
-                mm(col(pm, m, 2 * m), I, ln(xn), g2)
+                own = min(m, L - S - l0) if guests else m
+                for gp, c0, sgn in ((g1, 0, NI), (g2, m, I))[:1 if cfg["bx"][si] else 2]:
+                    mm(col(pm, c0, c0 + m), sgn, ln(xn), gp)
+                    mm(col(pm, c0, c0 + own), I, col(xc, l0, l0 + own), gp)
+                    if own < m:
+                        mm(col(pm, c0 + own, c0 + m), I, col(XT, TR + B, TR + B + S), gp)
                 act(ln(ad), col(pm, 0, m), ACT.Abs)
-                act(ln(bl), col(pm, m, 2 * m), ACT.Identity, 135.25, 0.5)
-                cn = bank(M1, m)
-                if cfg["naS"]:
-                    mm(cn, ONE, ln(thr), g3)
-                for b in range((l0 + m) // 16):
-                    c0 = max(l0, 16 * b)
-                    mm(col(cn, c0 - l0, m), BO, col(eq[b], c0, l0 + m), g3)
-                if cfg["naS"]:
-                    act(ln(na), cn, ACT.Sign)
+                c0 = 0 if cfg["bx"][si] else m
+                act(ln(bl), col(pm, c0, c0 + m), ACT.Identity, 159.75, 0.5)
+                pd = bank(M1, m)
+                if guests:
+                    mm(pd, I, ln(off2), g3)
                 else:
-                    tt(ln(na), cn, ln(thr), ALU.is_ge)
-            for q, l0, m, b0, b1 in ch:
+                    lower(pd, g3, nu, nf, nb, EQ[0])
+                mm(pd, BO, ln(ad), g3)
+                scan(ln(sd), col(R16, 0, m), pd, 0.0, ALU.add, ALU.max)
+                v = col(sd, l0 + 15, l0 + m, 16)
+                if cfg["tS"][si]:
+                    act(wr(vm), v, ACT.Relu, WAIT, -1.0)
+                    act(wr(th), v, ACT.Relu, -64 * (WAIT - U), 64.0)
+                else:
+                    ts(wr(vm), v, -WAIT, ALU.add, 0.0, ALU.min)
+                    ts(wr(th), v, WAIT, ALU.is_ge, BIG, ALU.mult)
+                if own < m:
+                    tt(col(vm, 9, 12), col(vm, 9, 12), lone, ALU.mult)
+                    tt(col(th, 9, 12), col(th, 9, 12), lone, ALU.mult)
+                tt(wr(ovr), wr(cB), wr(vm), ALU.subtract if cfg["tS"][si] else ALU.add)
+
+            def worst(q, l0, m, b0, b1):
                 ln = lambda a: col(a, l0, l0 + m)
                 wr = lambda a: col(a, b0, b1)
-                key, grp = bank(KB[q], 144, m), []
                 kx = col(kxs, 16 * l0, 16 * (l0 + m))
-                mm(key, col(ONE, 0, m), CI, grp)
-                mm(key, ln(kf), PAY, grp)
-                mm(col(key, 16, 144, 18), ln(ad), B8[1], grp)
-                o = mm(col(key, 17, 144, 18), ln(na), NA8, grp)
-                if cfg["ncS"]:
-                    mm(col(key, 16, 144, 18), ln(ncr), P8, grp)
-                    mm(col(key, 17, 144, 18), ln(ncr), P8, grp)["after"].append(o)
-                else:
-                    mm(key, ln(ncr), P0, grp)["after"].append(o)
-                last = distances(q, m, kx, ln(xn), 1, cfg["nve"][si], key, grp, EL[q][0], int(m * cfg["sub"]) // 2 * 2)
-                mm(key, ln(ne), NEm, grp)["after"].extend(last)
-                pick(q, m, key, None if live is None or (guests and q == 0) else wr(ovr), wr(wi))
+                nvs = {0: cfg["nve"][si][q]}
+                lq = cfg["late"][q]
+                if cfg["share"] and not (si == 1 and lq or si == 3 and lq == 2 or si == 2 and lq == 1 and q == 0):
+                    nvs[1] = cfg["nvs"][si][q]
+                keys, grp, sums = open_keys(q, m, kx, ln(kf), nvs)
+                both[q] = (keys, grp, []) if 1 in nvs else None
+                key = col(keys, 0, 128)
+                distances(q, m, kx, ln(xn), 1, nvs[0], key, grp, sums, EL[q][0], cfg["rep"][0],
+                          int(m * cfg["sub"][si]) // 2 * 2)
+                pick(0, q, m, key, wr(ovr), wr(wi))
+                if one & 8:
+                    if q == 0:
+                        return
+                    ln, wr = (lambda a: a), al
                 ts(wr(oi), wr(wi), 2047, ALU.bitwise_and)
                 cp(wr(ou), wr(oi))
-                act(ln(xo), ind(xw, wr(ou)), ACT.Identity, -7.5)
-            ts(al(sj), al(wi), 11, ALU.arith_shift_right, 31, ALU.bitwise_and)
-            cp(al(su), al(sj))
-            act(mask, ind(E, al(su)), ACT.Identity)
-            if guests:
-                tt(al(nz), al(nf), al(live), ALU.mult)
-            ts(al(nB), al(nz if guests else nf), U, ALU.add)
-            ts(al(hh), al(wi), U, ALU.add, 32.0, ALU.mult)
-            tt(al(sov), al(hh), al(nB), ALU.min)
-            ts(al(qi), al(wi), 32768, ALU.bitwise_and)
-            tt(al(a1), al(nf), al(qi), ALU.subtract)
-            tt(al(a2), al(a1), al(lm), ALU.max)
-            ts(al(wu), al(a2), float(TR), ALU.add)
-            tt(ind(col(XT, 0, TR + NW), al(wu)), bl, col(c128, 0, Lr), ALU.add)
-            ts(al(zi), al(wi), 19, ALU.arith_shift_right, 63, ALU.bitwise_and)
-            ts(al(live2), al(zi), 31.0, ALU.is_ge)
+                act(ln(xo), ind(xw1 if guests and l0 + m <= L - S else xw, wr(ou)))
+
+            def marks(l0, m):
+                b0, b1 = l0 // 16, (l0 + m) // 16
+                wr = lambda a: col(a, b0, b1)
+                ts(wr(fq), wr(wi), 31 << 11, ALU.bitwise_and)
+                ts(wr(su), wr(fq), 1.0 / 2048, ALU.mult)
+                act(col(mask, l0, l0 + m), ind(E, wr(su)))
+                ts(wr(hh), wr(wi), 32.0, ALU.mult)
+                if step == 0:
+                    tt(wr(a1), wr(nf), wr(th), ALU.min)
+                    tt(wr(keep), wr(a1), wr(blank), ALU.max)
+                tt(wr(sov), wr(hh), wr(keep), ALU.min)
+
+            def nearest(q, l0, m, b0, b1, si=si, step=step, kxs=kxs, kf=kf, xo=xo, mask=mask, sov=sov, ni=ni, nj=nj,
+                        nu2=nu2, both=both):
+                ln = lambda a: col(a, l0, l0 + m)
+                wr = lambda a: col(a, b0, b1)
+                kx = col(kxs, 16 * l0, 16 * (l0 + m))
+                if both[q]:
+                    keys, grp, sums = both[q]
+                else:
+                    keys, grp, sums = open_keys(q, m, kx, ln(kf), {1: cfg["nvs"][si][q]})
+                key = col(keys, 128, 256)
+                distances(q, m, kx, ln(xo), -1, cfg["nvs"][si][q], key, grp, sums, EL[q][1], cfg["rep"][1])
+                mm(key, ln(mask), I8, grp)
+                pick(1, q, m, key, wr(sov), wr(ni))
+                ts(wr(nj), wr(ni), 4095, ALU.bitwise_and)
+                cp(wr(nu2), wr(nj))
+
             if step == 1:
-                inc, xs_, b1_, pu = new("b", 12), new("b", Lr), new("f", 12), new("u", 12)
-                scan(al(inc), col(ONE, 0, nb), al(live2), 0.0, ALU.mult, ALU.add)
+                dd = new("f", 12)
+                ts(al(dd), al(nf), float(TR), ALU.is_lt, BIG, ALU.mult)
+                tt(al(a1), al(z0), al(dd), ALU.min)
+                tt(al(keep), al(a1), al(nf), ALU.max)
+            if not guests:
+                stays(0, Lr)
+            for c in ch:
+                if guests:
+                    if c[0] == 1:
+                        for k in range(2):
+                            if cfg["late"][k] == 1:
+                                late[k][0](*late[k][1])
+                    stays(c[1], c[2])
+                worst(*c)
+                if not cfg["mg"][si]:
+                    marks(c[1], c[2])
+            if cfg["mg"][si]:
+                marks(0, Lr)
+            a3 = new("f", 12)
+            tt(al(a3), al(nf), al(fq), ALU.min)
+            tt(al(a2), al(a3), al(lanew), ALU.max)
+            cp(al(wu), al(a2))
+            tt(ind(col(XT, 0, TR + NW), al(wu)), bl, x160, ALU.add)
+            if step == 1:
+                live, inc, xs_, b1_, pu = new("b", 12), new("b", 12), new("b", Lr), new("f", 12), new("u", 12)
+                tt(al(live), al(wi), al(th), ALU.is_lt)
+                scan(al(inc), al(ONE), al(live), 0.0, ALU.mult, ALU.add)
                 pp, gp = bank(M1, 16), []
-                mm(col(pp, 0, nb), TRI, al(live2), gp)
+                mm(col(pp, 0, nb), TRI, al(live), gp)
                 mm(col(pp, 1, nb), BO, col(inc, 0, nb - 1), gp)
                 if rnd == 0:
                     mm(col(pp, 12, 13), BO, col(inc, nb - 1, nb))
                 tt(al(b1_), col(pp, 0, nb), al(tr2), ALU.min)
-                ts(al(pu), al(b1_), 4096.0, ALU.add)
-                act(xs_, ind(xw, al(ou)), ACT.Identity)
+                ts(al(pu), al(b1_), 1.0 / U, ALU.mult, 512.0, ALU.add)
+                act(xs_, ind(xw, al(ou)))
                 cp(ind(SB[rnd], al(pu)), xs_)
                 if rnd == 0:
-                    cp(col(SB[0], S, S + 1), col(pp, 12, 13))
+                    ts(col(SB[0], S, S + 1), col(pp, 12, 13), 1.0 / U, ALU.mult)
                 w = 64 if rnd == 0 else S
                 tok = ("tok%d" % rnd, 0, 128, 0, 1, 1)
-                st["send%d" % rnd] = add("G", "send", (rnd, col(SB[rnd], 0, w)), tok, [col(SB[rnd], 0, w)], 300.0,
+                st["send%d" % rnd] = add("G", "send", (rnd, col(SB[rnd], 0, w)), tok, [col(SB[rnd], 0, w)], ("fix", 300.0),
                                          dur=1500.0, sem="snt%d" % rnd)
-            pa, pb, ga_, gb_ = bank(M1, Lr), bank(M0, Lr), [], []
-            bb, nl = new("f", Lr), new("i", Lr)
-            mm(pb, IF if cfg["ncS"] else IH, ncr, gb_)
-            mm(pb, I4, mask, gb_)
+            pa, ga_ = bank(M1, Lr), []
+            if cfg["cS"][si]:
+                pb, gb_ = bank(M0, Lr), []
+                mm(pb, IF, crep, gb_)
+                mm(pb, I, mask, gb_)
+                act(cm, pb)
+            else:
+                tt(cm, ind(ids, al(cu)), mask, ALU.add)
             mm(pa, IH, kf, ga_)
-            mm(pa, I4, mask, ga_)
-            act(bb, pb, ACT.Identity, 4096.0, -1.0)
-            tt(nl, pa, bb, ALU.min)
+            mm(pa, NI, mask, ga_)
+            tt(nl, pa, cm, ALU.max)
             cp(ind(col(CT, 0, TR + NW), al(wu)), nl)
-            for q, l0, m, b0, b1 in ch:
-                ln = lambda a: col(a, l0, l0 + m)
-                wr = lambda a: col(a, b0, b1)
-                key, grp = bank(KB[q], 144, m), []
-                kx = col(kxs, 16 * l0, 16 * (l0 + m))
-                mm(key, col(ONE, 0, m), CI, grp)
-                mm(key, ln(kf), PAY, grp)
-                distances(q, m, kx, ln(xo), -1, cfg["nvs"][si], key, grp, EL[q][1])
-                mm(key, ln(mask), NEm, grp)
-                pick(q, m, key, wr(sov), wr(ni))
-                ts(wr(nj), wr(ni), 2047, ALU.bitwise_and)
-                cp(wr(nu2), wr(nj))
+            if si == 3:
+                for k in range(2):
+                    if cfg["late"][k] == 2:
+                        late[k][0](*late[k][1])
+            for c in ch:
+                if si == 1 and cfg["late"][c[0]]:
+                    late[c[0]] = (nearest, c)
+                else:
+                    nearest(*c)
+            if si == 3:
+                for k in range(2):
+                    if cfg["late"][k] == 3:
+                        late[k][0](*late[k][1])
             if step == 0:
                 cp(al(nf2), al(nj))
+                ts(al(cB2), al(oi), 250 * U, ALU.add)
             else:
                 land = col(XT, TR + B, TR + B + 64) if rnd == 0 else LB
-                o = add("X", "arrive", (rnd,), land, [], 0.0, dur=cfg["hop"], sem="arr%d" % rnd)
+                o = add("X", "arrive", (rnd,), land, [], ("fix", 0.0), dur=cfg["hop"], sem="arr%d" % rnd)
                 o["soft"] = st["send%d" % rnd]
-            nu, nf, cu, live = nu2, nf2, ou, live2
+            nu, nf, cu, cB = nu2, nf2, ou, cB2
     yf = new("f", 2 * L)
-    cw = col(CT, TR, TR + B + S)
+    ms(col(XT, TR, TR + 1), 0.0)
     o = dma("Y", dr("yx", 0, B + S), col(XT, TR, TR + B + S), 3000.0, "st0")
     o["after"].append(st["send1"])
     dma("Y", dr("yx", B + S, B + 2 * S), LB, 2000.0, "st1")
     for t in range(2):
-        cp(col(yf, t * L, t * L + L), ind(cw, col(nend, 12 * t, 12 * t + 12)))
+        cp(col(yf, t * L, t * L + L), ind(CT, col(nend, 12 * t, 12 * t + 12)))
         dma("S", dr("yl", t * L, t * L + L), col(yf, t * L, t * L + L), 2000.0, "st%d" % (2 + t))
     return ops, top
 
@@ -471,16 +584,20 @@ def link(ops):
             seen.setdefault(a[0], []).append((o, a, w))
         for p in o["after"]:
             (order if p["eng"] == "P" and o["eng"] == "P" else deps).add(p["n"])
+        if "behind" in o:
+            order.add(o["behind"]["n"])
         if o["kind"] == "arrive":
             deps = set()
         o["deps"], o["order"] = deps, order - deps
 
 
 def schedule(ops, cfg):
-    lat = cfg["lat"]
     n = len(ops)
-    pre = [[(d, lat) for d in o["deps"]] + [(d, 0.0) for d in o["order"]] for o in ops]
+    more = {"P": cfg.get("latp", 0), "S": cfg.get("latS", 0)}
+    lat = lambda p, o: (cfg.get("lats", cfg["lat"]) if p["eng"] == o["eng"] else cfg["lat"]) + more.get(p["eng"], 0)
+    pre = [[(d, lat(ops[d], o)) for d in o["deps"]] + [(d, -ops[d].get("dur", 0.0)) for d in o["order"]] for o in ops]
     for o in ops:
+        o["cost"] = cost(o, cfg)
         if "soft" in o:
             pre[o["n"]].append((o["soft"]["n"], 0.0))
     suc = [[] for _ in ops]
@@ -549,12 +666,12 @@ def plan(cfg):
     for o in queues["P"]:
         gr = o["grp"]
         o["start"] = gr is None or gr[0] is o
-        o["stop"] = gr is None or max(pos[p["n"]] for p in gr) == pos[o["n"]]
+        o["stop"] = gr is None or max(pos[p["n"]] for p in gr if p) == pos[o["n"]]
     return ops, top, queues, total, end
 
 
 PLAN = plan(CFG)
-SCRATCH = {"xt": ("sbuf", [128, 2048], "bfloat16"), "ct": ("sbuf", [128, 2032], "int32"),
+SCRATCH = {"xt": ("sbuf", [128, TR + B + 64], "bfloat16"), "ct": ("sbuf", [128, TR + B + S], "int32"),
            "sb0": ("sbuf", [128, 2 * L], "bfloat16"), "sb1": ("sbuf", [128, 2 * L], "bfloat16"),
            "lb": ("dram", [128, S], "bfloat16"),
            "rb0": ("sbuf", [128, 64], "bfloat16"), "rb1": ("dram", [128, S], "bfloat16")}
@@ -641,8 +758,6 @@ def rank_program(g, core, T, topo):
                 r = q.memset(a[0], a[1])
             elif k == "scan":
                 r = q.tensor_tensor_scan(*a)
-            elif k == "red":
-                r = q.tensor_reduce(a[0], a[1], AxisListType.X, ALU.add)
             elif k == "act":
                 r = q.activation(a[0], a[1], a[2], bias=a[3], scale=a[4])
             elif k == "mm":

@@ -5,16 +5,16 @@ ACT = ActivationFunctionType
 B, L, S, N = 1792, 192, 48, 8
 TR = 2 * L
 U = 65536.0
-WAIT = 505 * U
 BIG = 2.0 ** 26
 CLS = (0, 4, 2, 6, 1, 5, 3, 7)
-CFG = {"blocks": (((0, 64), (64, 80)), ((0, 96), (96, 96))),
-       "nve": ((8, 8), (8, 8), (6, 8), (8, 8)), "nvs": ((8, 8), (6, 6), (6, 6), (6, 2)),
-       "gv": ((0.67, 0.0), (0.33, 0.5), (0.25, 0.25), (0.0, 0.25)), "sub": (0.5, 0.5, 0, 0.5),
-       "cS": (1, 0, 1, 1), "late": (0, 1), "mg": (1, 1, 1, 1), "neng": 8,
-       "bx": (0, 2, 2, 0), "tS": (0, 0, 0, 0), "share": 0, "rep": (4, 4), "xf": 1, "one": (6, 4, 7, 4),
-       "look": 400.0, "alpha": 60.0, "lat": 170.0, "lats": 210.0, "latp": 30.0, "latS": 60.0, "cyc": 0.83, "pe": 0.33,
-       "g": 1.3, "sc": 2.8, "vfix": 12.0, "mn": 25, "vr": 0.7, "sfix": 200.0, "ldc": 3400.0, "ldx": 3700.0, "hop": 3000.0}
+CFG = {"blocks": (((0, 96), (96, 48)), ((0, 96), (96, 96))),
+       "nve": ((8, 8), (8, 8), (8, 8), (8, 8)), "nvs": ((8, 6), (4, 6), (6, 4), (6, 2)),
+       "gv": ((0.33, 0.33), (0.125, 0.33), (0.25, 0.25), (0.0, 0.33)), "sub": (0.5, 0.5, 0, 0.5),
+       "cS": (2, 2, 2, 2), "late": (0, 1), "mg": (1, 1, 0, 1), "neng": 8,
+       "bx": (0, 2, 1, 0), "rep": (4, 2), "one": (2, 2, 5, 4), "con": 1276,
+       "onV": (0, 0, 0, 0), "spl": (0, 2, 0, 0), "pw": (0, 1, 1, 1),
+       "look": 60.0, "alpha": 20.0, "lat": 170.0, "lats": 210.0, "latp": 30.0, "latS": 60.0, "cyc": 0.83, "pe": 0.33,
+       "g": 1.3, "sc": 2.8, "vfix": 12.0, "mn": 25, "vr": 0.7, "sfix": 200.0, "ldx": 3700.0, "hop": 3000.0}
 DT = {"f": "float32", "b": "bfloat16", "i": "int32", "u": "uint16", "h": "float16"}
 
 
@@ -22,8 +22,8 @@ def col(a, c0, c1, step=1):
     return (a[0], a[1], a[2], a[3] + c0, a[3] + c1, step)
 
 
-def par(a, p):
-    return (a[0], 0, p, a[3], a[4], a[5])
+def rows(a, p0, p1):
+    return (a[0], p0, p1) + a[3:]
 
 
 def width(a):
@@ -42,7 +42,7 @@ def cost(o, cfg):
     if kind == "fix":
         return n
     if kind == "pe":
-        return cfg.get("pfix", 0) + n * cfg["pe"]
+        return n * cfg["pe"]
     if kind == "g":
         return 130 + 2 * n * cyc
     if kind == "gather":
@@ -50,8 +50,8 @@ def cost(o, cfg):
     if kind == "scatter":
         return 50 + cfg["sc"] * n * cyc
     if o["kind"] == "tt" and "ps" in (o["args"][1][0][:2], o["args"][2][0][:2]):
-        n = n * cfg.get("vr", 1)
-    return cfg["vfix" if o["eng"] == "V" else "sfix"] + max(cfg.get("mn", 64), n) * cyc
+        n = n * cfg["vr"]
+    return cfg["vfix" if o["eng"] == "V" else "sfix"] + max(cfg["mn"], n) * cyc
 
 
 def build(cfg):
@@ -120,6 +120,11 @@ def build(cfg):
             grp.append(o)
         return o
 
+    def chain(terms):
+        gp = []
+        for t in terms:
+            mm(*t, gp)["after"] += gp[-2:-1]
+
     def iota(out, pat, base=0, cm=0):
         return add("G", "iota", (out, pat, base, cm), out, [], ("g", width(out)))
 
@@ -131,127 +136,134 @@ def build(cfg):
     dr = lambda nm, a, b: (nm, 0, 128, a, b, 1)
 
     eni, joi = new("i", 24), new("i", 18)
-    if cfg["xf"] == 2:
-        dma("Y", eni, dr("en", 0, 24), 2000.0, "ld0")
-        dma("Y", col(CT, TR, TR + B), dr("ch", 0, B), cfg["ldc"], "ld1")
-        dma("S", joi, dr("jo", 0, 18), 2000.0, "ld2")
-        dma("S", col(XT, TR, TR + B), dr("x", 0, B), cfg["ldx"], "ld3")
-        ms(col(XT, TR, TR + 1), 31.0)
-    elif cfg["xf"]:
-        dma("S", eni, dr("en", 0, 24), 2000.0, "ld0")
-        dma("S", joi, dr("jo", 0, 18), 2000.0, "ld2")
-        o = dma("Y", col(XT, TR, TR + B), dr("x", 0, B), 1500 + (cfg["ldx"] - 1500) / 3, "ld3")
-        dma("Y", col(CT, TR, TR + B), dr("ch", 0, B), cfg["ldx"], "ld1")["behind"] = o
-        ms(col(XT, TR, TR + 1), 31.0)
-    else:
-        ms(col(XT, TR, TR + 1), 31.0)
-        dma("Y", eni, dr("en", 0, 24), 2000.0, "ld0")
-        dma("Y", col(CT, TR, TR + B), dr("ch", 0, B), cfg["ldc"], "ld1")
-        dma("S", joi, dr("jo", 0, 18), 2000.0, "ld2")
-        dma("S", col(XT, TR + 1, TR + B), dr("x", 1, B), cfg["ldx"], "ld3")["after"].append(ops[0])
+    dma("S", eni, dr("en", 0, 24), 2000.0, "ld0")
+    dma("S", joi, dr("jo", 0, 18), 2000.0, "ld2")
+    o = dma("Y", col(XT, TR, TR + B), dr("x", 0, B), 1500 + (cfg["ldx"] - 1500) / 3, "ld3")
+    dma("Y", col(CT, TR, TR + B), dr("ch", 0, B), cfg["ldx"], "ld1")["behind"] = o
+    ms(col(XT, TR, TR + 1), 31.0)
 
     pi, t_i = new("i", 1), new("i", 2)
     idt, ids = new("f", 256), new("f", TR + B + S)
-    JB, JR = new("f", 128), new("f", L)
+    JB, JR, G18 = new("f", 128), new("f", L), new("f", 144)
     iota(pi, [[0, 1]], 0, 1)
     iota(idt, [[1, 256]])
     iota(JB, [[1, 8], [0, 16]])
     iota(JR, [[0, 12], [1, 16]])
-    iota(col(CT, 0, TR), [[0, TR]])
-    iota(col(CT, TR + B, TR + B + S), [[0, S]])
-    ms(col(XT, 0, TR), 0.0)
-    act(col(ids, 0, 256), idt, ACT.Identity, -4096.0)
-    if cfg["xf"]:
-        ts(col(ids, 256, 512), idt, 256 - 4096.0, ALU.add)
-        for a, b, on_s in ((512, 1024, 1), (1024, 1536, 0), (1536, 2048, 1), (2048, TR + B + S, 0)):
-            if on_s:
-                act(col(ids, a, b), col(ids, 0, b - a), ACT.Identity, float(a))
-            else:
-                ts(col(ids, a, b), col(ids, 0, b - a), float(a), ALU.add)
+    iota(G18, [[1, 8], [0, 18]])
+    G40 = new("f", 40)
+    iota(G40, [[0, 5], [1, 8]])
+    if cfg["con"] >> 10 & 1:
+        iota(col(CT, 0, TR), [[0, TR]])
     else:
-        for a, b in ((256, 512), (512, 1024), (1024, 2048), (2048, TR + B + S)):
+        ms(col(CT, 0, TR), 0)
+    ms(col(CT, TR + B, TR + B + S), 0)
+    ms(col(XT, 0, TR), 0.0)
+
+    def fill(out, v):
+        return act(out, col(idt, 0, width(out)), ACT.Identity, v, 0.0)
+
+    def scale(k, out, a, v):
+        return act(out, a, ACT.Identity, 0.0, v) if cfg["con"] >> k & 1 else ts(out, a, v, ALU.mult)
+
+    def const(k, out, v):
+        return fill(out, v) if cfg["con"] >> k & 1 else ms(out, v)
+
+    act(col(ids, 0, 256), idt, ACT.Identity, -4096.0)
+    ts(col(ids, 256, 512), idt, 256 - 4096.0, ALU.add)
+    for a, b, on_s in ((512, 1024, 1), (1024, 1536, 0), (1536, 2048, 1), (2048, TR + B + S, 0)):
+        if on_s:
             act(col(ids, a, b), col(ids, 0, b - a), ACT.Identity, float(a))
+        else:
+            ts(col(ids, a, b), col(ids, 0, b - a), float(a), ALU.add)
 
     cols = new("f", 8)
-    pc, gcol, rc, sfE, sfS, r31 = [col(cols, j, j + 1) for j in range(6)]
+    pc, gcol, rc, r23, p18 = [col(cols, j, j + 1) for j in range(5)]
     cp(pc, pi)
     ts(col(t_i, 0, 1), pi, 4, ALU.arith_shift_right)
     ts(col(t_i, 1, 2), pi, 15, ALU.bitwise_and)
     cp(col(cols, 1, 3), t_i)
-    ts(r31, rc, -1.0, ALU.mult, 31.0, ALU.add)
+    ts(r23, rc, -1.0, ALU.mult, 23.0, ALU.add)
+    ts(p18, gcol, 2.0, ALU.mult, pc, ALU.add)
     I, NI, I8, BO, NBO, TRI, t1 = [new("b", 128) for _ in range(7)]
-    IH2 = new("h", 256)
-    IH = col(IH2, 0, 128)
-    M16, R16, OFF = new("f", L), new("f", L), new("b", L)
+    IH, M16, OFF = new("h", 128), new("f", L), new("b", L)
     ts(I, col(idt, 0, 128), pc, ALU.is_equal)
-    act(NI, I, ACT.Identity, 0.0, -1.0)
-    act(I8, I, ACT.Identity, 0.0, -8192.0)
+    scale(0, NI, I, -1.0)
+    scale(1, I8, I, -8192.0)
     cp(IH, I)
-    cp(col(IH2, 128, 256), I)
     ts(BO, JB, gcol, ALU.is_equal, U, ALU.mult)
-    act(NBO, BO, ACT.Identity, 0.0, -1.0)
+    scale(2, NBO, BO, -1.0)
     ts(M16, JR, rc, ALU.is_equal)
-    act(OFF, M16, ACT.Identity, -2.0 ** 36, 5 * 2.0 ** 34)
+    act(OFF, M16, ACT.Identity, -2.0 ** 20, 5 * 2.0 ** 18)
     add("G", "sel", (t1, BO, [[1, 128]], ALU.is_gt, 0.0, 0, -1), t1, [BO], ("g", 148))
     add("G", "sel", (TRI, t1, [[1, 128]], ALU.not_equal, -512 * U, 0, -1), TRI, [t1], ("g", 148))
-    B8f, RH, BK = new("f", 8), new("f", 8), new("b", 32)
-    B8 = {}
+    B8f, RH, B16, B8 = new("f", 8), new("f", 40), new("f", 8), {}
     ts(B8f, col(idt, 0, 8), gcol, ALU.is_equal)
-    ts(RH, B8f, col(B8f, 7, 8), ALU.add)
-    for k, v in enumerate((1, -1, 2, -2)):
-        B8[v] = col(BK, 8 * k, 8 * k + 8)
+    ts(RH, G40, gcol, ALU.is_equal, col(B8f, 7, 8), ALU.max)
+    ts(col(RH, 16, 32), col(RH, 16, 32), -1.0, ALU.mult)
+    for v in (1, -1, 2, -2):
+        B8[v] = new("b", 8)
         ts(B8[v], B8f, v * U, ALU.mult)
-    if 1 in cfg["cS"]:
+    if 2 in cfg["cS"]:
         IF = new("f", 128)
         act(IF, I)
-    act(R16, JR, ACT.Identity, 0.0, 0.0)
-    ms(col(R16, 0, L, 16), -2.0 ** 40)
-    RK = [new("f", 128) for _ in range(2)]
-    act(RK[0], col(R16, 0, 128), ACT.Identity, 2048.0)
-    act(RK[1], col(R16, 0, 128), ACT.Identity, 4096.0)
-    xoff = new("u", 8)
-    ts(xoff, col(idt, 0, 8), 16.0, ALU.mult, 15.0, ALU.add)
+        ts(B16, B8f, 1.0 / 16, ALU.mult)
+    PAY, P0 = new("h", 144), new("h", 144)
+    CK, BX = new("b", 144), new("b", 144)
+    ts(PAY, col(idt, 0, 144), p18, ALU.is_equal)
+    ts(BX, G18, gcol, ALU.is_equal, U, ALU.mult)
+    ms(CK, 0.0)
+    if min(cfg["cS"]) < 2:
+        cp(P0, CK)
+    for c in (16, 17):
+        ms(col(BX, c, 144, 18), 0.0)
+        if min(cfg["cS"]) < 2:
+            ts(col(P0, c, 144, 18), B8f, 1.0 / 16, ALU.mult)
+    for c in (16, 17):
+        ms(col(CK, c, 144, 18), -250 * U)
+    RK = [new("f", 144), new("f", 128)]
+    const(3, RK[0], 2048.0)
+    ms(col(RK[0], 0, 144, 18), -2.0 ** 40)
+    ms(col(RK[0], 16, 144, 18), 16384 - 251 * U)
+    ms(col(RK[0], 17, 144, 18), 0.0)
+    const(4, RK[1], 4096.0)
+    ms(col(RK[1], 0, 128, 16), -2.0 ** 40)
+    xoff = [new("u", 8), new("u", 8)]
+    ts(xoff[0], col(idt, 0, 8), 18.0, ALU.mult, 17.0, ALU.add)
+    ts(xoff[1], col(idt, 0, 8), 16.0, ALU.mult, 15.0, ALU.add)
+    CR = new("b", 24)
+    for j, v in enumerate((1.5 * 2.0 ** 34, 1.5 * 2.0 ** 39, 1.5 * 2.0 ** 35)):
+        ms(col(CR, 8 * j, 8 * j + 8), v)
     lanew, blank, tr2 = new("f", 12), new("f", 12), new("f", 12)
     ts(lanew, col(idt, 0, L, 16), rc, ALU.add)
     ts(blank, lanew, float(L), ALU.add)
     ts(tr2, lanew, L - 512.0, ALU.add, U, ALU.mult)
     E, c160, ONE = new("b", 32), new("b", L), new("b", 12)
-    ts(E, col(idt, 0, 32), r31, ALU.is_equal, 4096.0, ALU.mult)
+    ts(E, col(idt, 0, 32), r23, ALU.is_equal, 4096.0, ALU.mult)
     if 0 in cfg["bx"]:
-        act(c160, JR, ACT.Identity, -160.0, 0.0)
+        const(5, c160, -160.0)
     ms(ONE, 1.0)
-    SB = [("sb%d" % t, 0, 128, 0, 2 * L, 1) for t in range(2)]
+    SB = [("sb%d" % t, 0, 128, 0, 2 * L + 16, 1) for t in range(2)]
     for t in range(2):
-        act(col(SB[t], 0, 64), col(idt, 0, 64), ACT.Identity, 0.0, 0.0)
-    SC = []
-    for v in (16 * 2048 - 256 * U, TR - U):
-        sc = new("f", 256)
-        act(sc, idt, ACT.Identity, v, 0.0)
-        SC.append([col(sc, 0, 128), col(sc, 128, 256)])
+        ms(col(SB[t], 0, 64), 0.0)
+    SC = [[new("f", w) for q in range(2)] for w in (144, 128)]
+    for k in range(2):
+        for q in range(2):
+            if cfg["con"] >> (8 + k) & 1:
+                iota(SC[k][q], [[0, width(SC[k][q])]], -5 * 65536 - 16384 - 1023)
+            else:
+                const(6 + k, SC[k][q], -5 * U - 16384 - 1023)
     nend = new("u", 24)
     ms(col(nend, 8, 12), TR)
 
     KX = [new("b", 16 * L) for _ in range(3)]
-    EL = [[new("b", 16 * 112) for _ in range(2)] for _ in range(2)]
+    EL = [[new("b", 16 * 96) for _ in range(2)] for _ in range(2)]
     EQ = [new("b", 1248) for _ in range(2)]
     AX = [new("f", 128) for _ in range(2)]
     KB, XB, DB, M0, M1 = (0, 1), (2, 3), (4, 5), 6, 7
     dnext = [0]
     LB = ("lb", 0, 128, 0, S, 1)
 
-    def open_keys(q, m, kx, kfq, nvs):
-        keys, grp = bank(KB[q], 256, m), []
-        lo, hi = min(nvs), max(nvs) + 1
-        mm(col(keys, 128 * lo, 128 * hi), kfq, col(IH2, 128 * lo, 128 * hi), grp)
-        sums = []
-        for s in range(16):
-            use = [k for k in nvs if s % 8 in CLS[:nvs[k]]]
-            if use:
-                a, b = use[0], use[-1] + 1
-                sums.append(mm(col(keys, 128 * a + s, 128 * b, 16), col(kx, s, 16 * m, 16), col(BK, 8 * a, 8 * b), grp))
-        return keys, grp, sums
-
-    def distances(q, m, kx, xr, sg, nv, key, grp, sums, el, rep, cut=0):
+    def distances(q, m, kx, xr, sg, nv, key, grp, rep, cut=0, spl=0):
         def units(cs, r):
             us = []
             for c in cs:
@@ -259,8 +271,13 @@ def build(cfg):
                     continue
                 us += [(c, 4)] if r == 4 and c + 4 in cs else [(c, 8)] if r > 1 else [(c, 16), (c + 8, 16)]
             return us
+        W = width(key)
+        slot = lambda s: col(key, s, W, W // 8)
+        parts = ((0, spl), (spl, m)) if spl else ((0, m),)
+        sums = {(s, p0): mm(rows(slot(s), p0, p1), col(kx, 16 * p0 + s, 16 * p1, 16), B8[sg], grp)
+                for s in range(16) if s % 8 in CLS[:nv] for p0, p1 in parts}
         vs, ss = units(CLS[:nv], rep), units(CLS[nv:], 4)
-        xps, at = {}, 0
+        xps, at, el = {}, 0, EL[q][sg < 0]
         for r in sorted(set(16 // st for c, st in vs)):
             xps[r] = col(bank(XB[q], 512), at, at + r * m)
             at += r * m
@@ -285,43 +302,44 @@ def build(cfg):
                     if b > a:
                         tt(col(e, r * a, r * b), col(kx, 16 * a + c, 16 * b, st), col(xps[r], r * a, r * b), ALU.min)
             for j in range(r):
-                o = mm(col(key, c + st * j, 128, 16), col(e, j, r * m, r), B8[sg if on_s else -2 * sg], grp)
-                if not on_s:
-                    o["after"] += sums
-                    mins.append(o)
+                for p0, p1 in ((0, m),) if on_s else parts:
+                    o = mm(rows(slot(c + st * j), p0, p1), col(e, r * p0 + j, r * p1, r), B8[sg if on_s else -2 * sg], grp)
+                    if not on_s:
+                        o["after"].append(sums[c + st * j, p0])
+                        mins.append(o)
         at = 0
         for n in (8, 4, 2, 1):
             if nv & n:
-                c = CLS[at]
+                if sg < 0 or n >= 4:
+                    mm(col(key, CLS[at], W, 8 // n), xr, col(BX if sg > 0 else NBO, CLS[at], W, 8 // n), grp)["after"] += mins
+                else:
+                    for s in range(CLS[at], 16, 8 // n):
+                        mm(slot(s), xr, B8[1], grp)["after"] += mins
                 at += n
-                mm(col(key, c, 128, 8 // n), xr, col(BO if sg > 0 else NBO, c, 128, 8 // n), grp)["after"] += mins
 
-    def pick(k, q, m, key, ovr, wi):
-        scan(par(SC[k][q], m), par(RK[k], m), key, 0.0, ALU.add, ALU.max)
-        tt(AX[q], ind(SC[k][q], xoff), col(M16, 0, 128), ALU.mult)
-        w = bank(XB[q], m // 16)
-        mm(w, AX[q], col(RH, 0, m // 16))
-        tt(wi, w, ovr, ALU.max)
+    def best(k, q, m, key):
+        scan(rows(SC[k][q], 0, m), rows(RK[k], 0, m), key, 0.0, ALU.add, ALU.max)
+        tt(AX[q], ind(SC[k][q], xoff[k]), col(M16, 0, 128), ALU.mult)
 
-    def lower(pd, gp, nu, nf, nb, buf):
-        Lr, at = 16 * nb, 0
-        nrep = new("u", Lr)
+    def waits(bk, nu, nf, nb, buf):
+        Lr, at, pd, gp = 16 * nb, 0, bank(bk, 16 * nb), []
+        nrep, xw = new("u", Lr), new("b", Lr)
         ts(nrep, ind(ids, col(nu, 0, nb)), 4096.0, ALU.add)
         mm(pd, I, col(OFF, 0, Lr), gp)
         for b in range(nb):
             e = col(buf, at, at + Lr - 16 * b)
             at += Lr - 16 * b
-            ts(e, col(nrep, 16 * b, Lr), col(nf, b, b + 1), ALU.is_equal, 512.0, ALU.mult)
+            ts(e, col(nrep, 16 * b, Lr), col(nf, b, b + 1), ALU.is_equal, 512 / U, ALU.mult)
             mm(col(pd, 16 * b, 16 * b + 16), TRI, col(e, 0, 16), gp)
             if b + 1 < nb:
                 mm(col(pd, 16 * b + 16, Lr), BO, col(e, 16, Lr - 16 * b), gp)
+        ts(xw, pd, 500.0, ALU.min, 0.0, ALU.max)
+        return xw
 
-    nu0, nf0, off2 = new("u", 24), new("f", 24), new("b", L)
+    nu0, nf0, cu0 = new("u", 24), new("f", 24), new("u", 24)
     ts(nu0, eni, float(TR), ALU.add)
     ts(nf0, eni, float(TR), ALU.add)
-    lower(bank(DB[1], L), [], col(nu0, 12, 24), col(nf0, 12, 24), 12, EQ[1])
-    act(off2, bank(DB[1], L))
-    cu0, cB0 = new("u", 24), new("f", 24)
+    first = [waits(DB[t], col(nu0, 12 * t, 12 * t + 12), col(nf0, 12 * t, 12 * t + 12), 9 + 3 * t, EQ[t]) for t in range(2)]
     st = {}
     late = {}
     for rnd in range(2):
@@ -329,19 +347,21 @@ def build(cfg):
         nb = Lr // 16
         NW = B if rnd == 0 else B + S
         al = lambda a: col(a, 0, nb)
-        nu, nf, cu, cB = [col(a, 12 * rnd, 12 * rnd + 12) for a in (nu0, nf0, cu0, cB0)]
+        nu, nf, cu = [col(a, 12 * rnd, 12 * rnd + 12) for a in (nu0, nf0, cu0)]
         cp(col(cu, 0, 9), col(joi, 9 * rnd, 9 * rnd + 9))
-        ts(col(cB, 0, 9), col(joi, 9 * rnd, 9 * rnd + 9), 250 * U, ALU.add)
         z0 = nf
         if rnd == 1:
             ts(col(cu, 9, 12), col(lanew, 0, 3), float(B), ALU.add)
-            ts(col(cB, 9, 12), col(lanew, 0, 3), B + 250 * U, ALU.add)
             cnt = col(XT, TR + B + S, TR + B + S + 1)
-            lone, z0, zt = new("f", 3), new("f", 12), new("f", 3)
+            lone, z0, zt, idle = new("f", 3), new("f", 12), new("f", 3), new("b", S)
             cp(col(z0, 0, 9), col(nf, 0, 9))
             ts(lone, col(lanew, 0, 3), cnt, ALU.is_lt)
             tt(zt, col(nf, 9, 12), lone, ALU.mult)
             ts(col(z0, 9, 12), zt, float(TR), ALU.max)
+            k1, kd = new("f", S), new("f", S)
+            ts(k1, col(idt, 0, S), 1.0, ALU.add)
+            tt(kd, k1, col(M16, 0, S), ALU.mult)
+            ts(idle, kd, cnt, ALU.is_gt, 500.0, ALU.mult)
         for step in range(2):
             si = 2 * rnd + step
             guests = si == 2
@@ -349,13 +369,16 @@ def build(cfg):
             xw1, xw = col(XT, TR, TR + nw1), col(XT, TR, TR + NW)
             ku, kf = new("u", Lr), new("h", Lr)
             xn, xc, xo, ad, bl, mask = [new("b", Lr) for _ in range(6)]
-            wi, oi, fq, ni, nj = [new("i", 12) for _ in range(5)]
             ou, su, wu = new("u", 12), new("u", 12), new("u", 12)
-            vm, th, ovr, hh, sov, keep, a1, a2, cB2, nf2 = [new("f", 12) for _ in range(10)]
+            th, put, stay, keep, a1, a2, a3, a4, nf2 = [new("f", 12) for _ in range(9)]
+            wipe, held = new("b", 12), new("h", 12)
             nu2 = new("u", 12) if step == 0 else col(nend, 12 * rnd, 12 * rnd + 12)
-            sd, cm, nl = new("f", Lr), new("f", Lr), new("i", Lr)
+            cm, nl = new("f", Lr), new("i", Lr)
             kxs = KX[(0, 1, 0, 2)[si]]
             ch = [(q, l0, m, l0 // 16, (l0 + m) // 16) for q, (l0, m) in enumerate(cfg["blocks"][rnd])]
+            take = lambda bit, out, a, si=si: (cp if cfg["onV"][si] & bit else act)(out, a)
+            spl = [(32 if m <= 64 else 64) if cfg["spl"][si] >> q & 1 else 0 for q, l0, m, b0, b1 in ch]
+            cuts = [spl[q] or int(m * cfg["sub"][si]) // 2 * 2 for q, l0, m, b0, b1 in ch]
             one = cfg["one"][si]
             for q, l0, m, b0, b1 in ch:
                 ln = lambda a: col(a, l0, l0 + m)
@@ -365,25 +388,28 @@ def build(cfg):
                 elif q == 0:
                     cp(ku, ind(col(CT, 0, TR + nw1), al(nu)))
                 if not one & 2:
-                    act(ln(xn), ind(col(XT, 0, TR + nw1), wr(nu)))
+                    take(2, ln(xn), ind(col(XT, 0, TR + nw1), wr(nu)))
                 elif q == 0:
-                    act(xn, ind(col(XT, 0, TR + nw1), al(nu)))
+                    take(2, xn, ind(col(XT, 0, TR + nw1), al(nu)))
                 mv = int(round(m * cfg["gv"][si][q] / 2)) * 2
-                cut = max(mv, int(m * cfg["sub"][si]) // 2 * 2)
-                for a, b, eng in ((0, mv, cp), (mv, cut, act), (cut, m, act)):
+                cut = cuts[q]
+                for a, b in zip(sorted({0, mv, cut}), sorted({mv, cut, m} - {0})):
                     if b > a:
-                        eng(col(kxs, 16 * (l0 + a), 16 * (l0 + b)), ind(xw1, col(ku, l0 + a, l0 + b)))
+                        (cp if b <= mv else act)(col(kxs, 16 * (l0 + a), 16 * (l0 + b)), ind(xw1, col(ku, l0 + a, l0 + b)))
                 if not one & 4:
                     cp(ln(kf), ln(ku))
             if one & 4:
                 cp(kf, ku)
-            if cfg["cS"][si]:
+            if cfg["cS"][si] == 2:
                 crep = new("f", Lr)
-                act(crep, ind(ids, al(cu)))
-            if guests:
-                act(col(xc, 0, L - S), ind(xw1, col(cu, 0, 9)))
+                act(crep, ind(ids, al(cu)), ACT.Identity, 4096.0)
             else:
-                act(xc, ind(xw, al(cu)))
+                crep = new("h", Lr)
+                ts(crep, ind(ids, al(cu)), 4096.0, ALU.add)
+            if guests:
+                take(4, col(xc, 0, L - S), ind(xw1, col(cu, 0, 9)))
+            else:
+                take(4, xc, ind(xw, al(cu)))
             if cfg["bx"][si]:
                 x160 = new("b", Lr)
                 if cfg["bx"][si] == 1:
@@ -392,16 +418,14 @@ def build(cfg):
                     act(x160, xn, ACT.Identity, -160.0)
             else:
                 x160 = col(c160, 0, Lr)
-            both = {}
+            xwt = first[rnd] if step == 0 else waits(M1, nu, nf, nb, EQ[0])
 
-            def stays(l0, m):
-                b0, b1 = l0 // 16, (l0 + m) // 16
+            def blends(l0, m):
                 ln = lambda a: col(a, l0, l0 + m)
-                wr = lambda a: col(a, b0, b1)
                 pm = bank(M0, 2 * m)
-                g1, g2, g3 = [], [], []
                 own = min(m, L - S - l0) if guests else m
-                for gp, c0, sgn in ((g1, 0, NI), (g2, m, I))[:1 if cfg["bx"][si] else 2]:
+                for c0, sgn in ((0, NI), (m, I))[:1 if cfg["bx"][si] else 2]:
+                    gp = []
                     mm(col(pm, c0, c0 + m), sgn, ln(xn), gp)
                     mm(col(pm, c0, c0 + own), I, col(xc, l0, l0 + own), gp)
                     if own < m:
@@ -409,102 +433,100 @@ def build(cfg):
                 act(ln(ad), col(pm, 0, m), ACT.Abs)
                 c0 = 0 if cfg["bx"][si] else m
                 act(ln(bl), col(pm, c0, c0 + m), ACT.Identity, 159.75, 0.5)
-                pd = bank(M1, m)
-                if guests:
-                    mm(pd, I, ln(off2), g3)
-                else:
-                    lower(pd, g3, nu, nf, nb, EQ[0])
-                mm(pd, BO, ln(ad), g3)
-                scan(ln(sd), col(R16, 0, m), pd, 0.0, ALU.add, ALU.max)
-                v = col(sd, l0 + 15, l0 + m, 16)
-                if cfg["tS"][si]:
-                    act(wr(vm), v, ACT.Relu, WAIT, -1.0)
-                    act(wr(th), v, ACT.Relu, -64 * (WAIT - U), 64.0)
-                else:
-                    ts(wr(vm), v, -WAIT, ALU.add, 0.0, ALU.min)
-                    ts(wr(th), v, WAIT, ALU.is_ge, BIG, ALU.mult)
-                if own < m:
-                    tt(col(vm, 9, 12), col(vm, 9, 12), lone, ALU.mult)
-                    tt(col(th, 9, 12), col(th, 9, 12), lone, ALU.mult)
-                tt(wr(ovr), wr(cB), wr(vm), ALU.subtract if cfg["tS"][si] else ALU.add)
 
             def worst(q, l0, m, b0, b1):
                 ln = lambda a: col(a, l0, l0 + m)
                 wr = lambda a: col(a, b0, b1)
-                kx = col(kxs, 16 * l0, 16 * (l0 + m))
-                nvs = {0: cfg["nve"][si][q]}
-                lq = cfg["late"][q]
-                if cfg["share"] and not (si == 1 and lq or si == 3 and lq == 2 or si == 2 and lq == 1 and q == 0):
-                    nvs[1] = cfg["nvs"][si][q]
-                keys, grp, sums = open_keys(q, m, kx, ln(kf), nvs)
-                both[q] = (keys, grp, []) if 1 in nvs else None
-                key = col(keys, 0, 128)
-                distances(q, m, kx, ln(xn), 1, nvs[0], key, grp, sums, EL[q][0], cfg["rep"][0],
-                          int(m * cfg["sub"][si]) // 2 * 2)
-                pick(0, q, m, key, wr(ovr), wr(wi))
-                if one & 8:
-                    if q == 0:
-                        return
-                    ln, wr = (lambda a: a), al
-                ts(wr(oi), wr(wi), 2047, ALU.bitwise_and)
-                cp(wr(ou), wr(oi))
-                act(ln(xo), ind(xw1 if guests and l0 + m <= L - S else xw, wr(ou)))
+                key, grp = bank(KB[q], 144, m), []
+                mm(key, col(I, 0, m), CK, grp)
+                mm(key, ln(kf), PAY, grp)
+                if cfg["cS"][si] == 2:
+                    mm(col(key, 16, 144, 18), ln(crep), B16, grp)
+                    mm(col(key, 17, 144, 18), ln(crep), B16, grp)
+                else:
+                    mm(key, ln(crep), P0, grp)
+                mm(col(key, 16, 144, 18), ln(ad), B8[1], grp)
+                mm(col(key, 17, 144, 18), ln(xw_[q]), B8[1], grp)
+                distances(q, m, col(kxs, 16 * l0, 16 * (l0 + m)), ln(xn), 1, cfg["nve"][si][q], key, grp, cfg["rep"][0],
+                          cuts[q], spl[q])
+                best(0, q, m, key)
+                w = bank(XB[q], 24)
+                chain([(w, AX[q], col(RH, 16, 40)), (col(w, 0, 16), I, col(CR, 0, 16)), (col(w, 0, 16), NI, col(CR, 0, 16)),
+                       (col(w, 0, 16), AX[q], col(RH, 0, 16)), (col(w, 8, 16), I, col(CR, 0, 8)), (col(w, 8, 16), NI, col(CR, 0, 8))])
+                k = b1 - b0
+                ts(wr(ou), col(w, 0, k), 1023.0, ALU.add)
+                ts(wr(su), col(w, 8, 8 + k), 1.0 / 2048, ALU.mult, 8.0, ALU.add)
+                ts(wr(put), col(w, 8, 8 + k), 0.0, ALU.is_ge, 4096.0, ALU.mult)
+                ts(wr(stay), col(w, 16, 16 + k), -U / 2, ALU.is_ge)
+                ts(wr(wipe), col(w, 16, 16 + k), -U / 2, ALU.is_ge, 2.0 ** 36, ALU.mult)
+                ts(wr(th), col(w, 16, 16 + k), 242 * U, ALU.is_ge, BIG, ALU.mult)
+                take(1, ln(xo), ind(xw1 if guests and l0 + m <= L - S else xw, wr(ou)))
 
             def marks(l0, m):
                 b0, b1 = l0 // 16, (l0 + m) // 16
                 wr = lambda a: col(a, b0, b1)
-                ts(wr(fq), wr(wi), 31 << 11, ALU.bitwise_and)
-                ts(wr(su), wr(fq), 1.0 / 2048, ALU.mult)
-                act(col(mask, l0, l0 + m), ind(E, wr(su)))
-                ts(wr(hh), wr(wi), 32.0, ALU.mult)
+                take(8, col(mask, l0, l0 + m), ind(E, wr(su)))
                 if step == 0:
+                    if guests and b1 == nb:
+                        tt(col(th, 9, 12), col(th, 9, 12), lone, ALU.mult)
                     tt(wr(a1), wr(nf), wr(th), ALU.min)
                     tt(wr(keep), wr(a1), wr(blank), ALU.max)
-                tt(wr(sov), wr(hh), wr(keep), ALU.min)
+                    ts(wr(a4), wr(keep), -float(TR), ALU.add)
+                tt(wr(held), wr(a4), wr(stay), ALU.mult)
 
-            def nearest(q, l0, m, b0, b1, si=si, step=step, kxs=kxs, kf=kf, xo=xo, mask=mask, sov=sov, ni=ni, nj=nj,
-                        nu2=nu2, both=both):
+            def nearest(q, l0, m, b0, b1, si=si, step=step, kxs=kxs, kf=kf, xo=xo, mask=mask, wipe=wipe, held=held,
+                        nu2=nu2, nf2=nf2):
                 ln = lambda a: col(a, l0, l0 + m)
                 wr = lambda a: col(a, b0, b1)
-                kx = col(kxs, 16 * l0, 16 * (l0 + m))
-                if both[q]:
-                    keys, grp, sums = both[q]
-                else:
-                    keys, grp, sums = open_keys(q, m, kx, ln(kf), {1: cfg["nvs"][si][q]})
-                key = col(keys, 128, 256)
-                distances(q, m, kx, ln(xo), -1, cfg["nvs"][si][q], key, grp, sums, EL[q][1], cfg["rep"][1])
+                key, grp = bank(KB[q], 128, m), []
+                mm(key, ln(kf), IH, grp)
+                distances(q, m, col(kxs, 16 * l0, 16 * (l0 + m)), ln(xo), -1, cfg["nvs"][si][q], key, grp, cfg["rep"][1])
                 mm(key, ln(mask), I8, grp)
-                pick(1, q, m, key, wr(sov), wr(ni))
-                ts(wr(nj), wr(ni), 4095, ALU.bitwise_and)
-                cp(wr(nu2), wr(nj))
+                best(1, q, m, key)
+                k = b1 - b0
+                w, ax, c = bank(XB[q], k), rows(AX[q], 0, m), col(CR, 16, 16 + k)
+                chain([(w, ax, rows(col(RH, 16, 16 + k), 0, m)), (w, I, c), (w, NI, c), (w, ax, rows(col(RH, 0, k), 0, m)),
+                       (w, I, wr(wipe)), (w, NI, wr(wipe)), (w, IH, wr(held))])
+                ts(wr(nu2), w, float(TR), ALU.add)
+                if step == 0:
+                    ts(wr(nf2), w, float(TR), ALU.add)
 
             if step == 1:
                 dd = new("f", 12)
                 ts(al(dd), al(nf), float(TR), ALU.is_lt, BIG, ALU.mult)
                 tt(al(a1), al(z0), al(dd), ALU.min)
                 tt(al(keep), al(a1), al(nf), ALU.max)
-            if not guests:
-                stays(0, Lr)
+                ts(al(a4), al(keep), -float(TR), ALU.add)
+            xw_ = [xwt, xwt]
+            if guests:
+                xw_[1] = new("b", Lr)
+                cp(col(xw_[1], 96, L - S), col(xwt, 96, L - S))
+                tt(col(xw_[1], L - S, L), col(xwt, L - S, L), idle, ALU.max)
+            else:
+                blends(0, Lr)
             for c in ch:
                 if guests:
                     if c[0] == 1:
                         for k in range(2):
                             if cfg["late"][k] == 1:
                                 late[k][0](*late[k][1])
-                    stays(c[1], c[2])
+                    blends(c[1], c[2])
                 worst(*c)
                 if not cfg["mg"][si]:
                     marks(c[1], c[2])
             if cfg["mg"][si]:
                 marks(0, Lr)
-            a3 = new("f", 12)
-            tt(al(a3), al(nf), al(fq), ALU.min)
-            tt(al(a2), al(a3), al(lanew), ALU.max)
-            cp(al(wu), al(a2))
+            if cfg["pw"][si]:
+                for a in range(nb):
+                    ts(col(wu, a, a + 1), col(put, a, a + 1), col(nf, a, a + 1), ALU.min, col(lanew, a, a + 1), ALU.max)
+            else:
+                tt(al(a3), al(nf), al(put), ALU.min)
+                tt(al(a2), al(a3), al(lanew), ALU.max)
+                cp(al(wu), al(a2))
             tt(ind(col(XT, 0, TR + NW), al(wu)), bl, x160, ALU.add)
             if step == 1:
                 live, inc, xs_, b1_, pu = new("b", 12), new("b", 12), new("b", Lr), new("f", 12), new("u", 12)
-                tt(al(live), al(wi), al(th), ALU.is_lt)
+                tt(al(live), al(stay), al(th), ALU.is_le)
                 scan(al(inc), al(ONE), al(live), 0.0, ALU.mult, ALU.add)
                 pp, gp = bank(M1, 16), []
                 mm(col(pp, 0, nb), TRI, al(live), gp)
@@ -512,11 +534,15 @@ def build(cfg):
                 if rnd == 0:
                     mm(col(pp, 12, 13), BO, col(inc, nb - 1, nb))
                 tt(al(b1_), col(pp, 0, nb), al(tr2), ALU.min)
-                ts(al(pu), al(b1_), 1.0 / U, ALU.mult, 512.0, ALU.add)
-                act(xs_, ind(xw, al(ou)))
-                cp(ind(SB[rnd], al(pu)), xs_)
                 if rnd == 0:
+                    b2_, b3_ = new("f", 12), new("f", 12)
                     ts(col(SB[0], S, S + 1), col(pp, 12, 13), 1.0 / U, ALU.mult)
+                    ts(al(b2_), al(b1_), (S - 512) * U, ALU.is_ge, 16 * U, ALU.mult)
+                    tt(al(b3_), al(b1_), al(b2_), ALU.add)
+                    b1_ = b3_
+                ts(al(pu), al(b1_), 1.0 / U, ALU.mult, 512.0, ALU.add)
+                take(16, xs_, ind(xw, al(ou)))
+                cp(ind(SB[rnd], al(pu)), xs_)
                 w = 64 if rnd == 0 else S
                 tok = ("tok%d" % rnd, 0, 128, 0, 1, 1)
                 st["send%d" % rnd] = add("G", "send", (rnd, col(SB[rnd], 0, w)), tok, [col(SB[rnd], 0, w)], ("fix", 300.0),
@@ -524,9 +550,9 @@ def build(cfg):
             pa, ga_ = bank(M1, Lr), []
             if cfg["cS"][si]:
                 pb, gb_ = bank(M0, Lr), []
-                mm(pb, IF, crep, gb_)
+                mm(pb, IF if cfg["cS"][si] == 2 else IH, crep, gb_)
                 mm(pb, I, mask, gb_)
-                act(cm, pb)
+                act(cm, pb, ACT.Identity, -4096.0)
             else:
                 tt(cm, ind(ids, al(cu)), mask, ALU.add)
             mm(pa, IH, kf, ga_)
@@ -546,14 +572,11 @@ def build(cfg):
                 for k in range(2):
                     if cfg["late"][k] == 3:
                         late[k][0](*late[k][1])
-            if step == 0:
-                cp(al(nf2), al(nj))
-                ts(al(cB2), al(oi), 250 * U, ALU.add)
-            else:
+            if step == 1:
                 land = col(XT, TR + B, TR + B + 64) if rnd == 0 else LB
                 o = add("X", "arrive", (rnd,), land, [], ("fix", 0.0), dur=cfg["hop"], sem="arr%d" % rnd)
                 o["soft"] = st["send%d" % rnd]
-            nu, nf, cu, cB = nu2, nf2, ou, cB2
+            nu, nf, cu = nu2, nf2, ou
     yf = new("f", 2 * L)
     ms(col(XT, TR, TR + 1), 0.0)
     o = dma("Y", dr("yx", 0, B + S), col(XT, TR, TR + B + S), 3000.0, "st0")
@@ -593,8 +616,8 @@ def link(ops):
 
 def schedule(ops, cfg):
     n = len(ops)
-    more = {"P": cfg.get("latp", 0), "S": cfg.get("latS", 0)}
-    lat = lambda p, o: (cfg.get("lats", cfg["lat"]) if p["eng"] == o["eng"] else cfg["lat"]) + more.get(p["eng"], 0)
+    more = {"P": cfg["latp"], "S": cfg["latS"]}
+    lat = lambda p, o: cfg["lats" if p["eng"] == o["eng"] else "lat"] + more.get(p["eng"], 0)
     pre = [[(d, lat(ops[d], o)) for d in o["deps"]] + [(d, -ops[d].get("dur", 0.0)) for d in o["order"]] for o in ops]
     for o in ops:
         o["cost"] = cost(o, cfg)
@@ -609,22 +632,18 @@ def schedule(ops, cfg):
     for i in range(n - 1, -1, -1):
         prio[i] = span[i] + max([prio[j] + l for j, l in suc[i]] + [0.0])
     left = [len(p) for p in pre]
-    rdy = [0.0] * n
-    free = {}
-    queues = {}
+    rdy, free, queues, end = [0.0] * n, {}, {}, 0.0
     pool = [i for i in range(n) if left[i] == 0]
-    end = 0.0
     while pool:
         t0, e0 = min((max(rdy[i], free.get(ops[i]["eng"], 0.0)), ops[i]["eng"]) for i in pool)
         cand = [i for i in pool if ops[i]["eng"] == e0 and rdy[i] <= t0 + cfg["look"]]
         i = max(cand, key=lambda j: (prio[j] - cfg["alpha"] * max(0.0, rdy[j] - t0), -j))
         pool.remove(i)
         o = ops[i]
-        s = max(t0, rdy[i])
-        o["t"] = s
-        free[e0] = s + o["cost"]
+        o["t"] = max(t0, rdy[i])
+        free[e0] = o["t"] + o["cost"]
         queues.setdefault(e0, []).append(o)
-        fin = s + span[i]
+        fin = o["t"] + span[i]
         end = max(end, fin)
         for j, l in suc[i]:
             rdy[j] = max(rdy[j], fin + l)
@@ -666,13 +685,13 @@ def plan(cfg):
     for o in queues["P"]:
         gr = o["grp"]
         o["start"] = gr is None or gr[0] is o
-        o["stop"] = gr is None or max(pos[p["n"]] for p in gr if p) == pos[o["n"]]
+        o["stop"] = gr is None or max(pos[p["n"]] for p in gr) == pos[o["n"]]
     return ops, top, queues, total, end
 
 
 PLAN = plan(CFG)
 SCRATCH = {"xt": ("sbuf", [128, TR + B + 64], "bfloat16"), "ct": ("sbuf", [128, TR + B + S], "int32"),
-           "sb0": ("sbuf", [128, 2 * L], "bfloat16"), "sb1": ("sbuf", [128, 2 * L], "bfloat16"),
+           "sb0": ("sbuf", [128, 2 * L + 16], "bfloat16"), "sb1": ("sbuf", [128, 2 * L + 16], "bfloat16"),
            "lb": ("dram", [128, S], "bfloat16"),
            "rb0": ("sbuf", [128, 64], "bfloat16"), "rb1": ("dram", [128, S], "bfloat16")}
 for _k in "fbiuh":

from concourse.mybir import AluOpType, AxisListType, ActivationFunctionType

ALU = AluOpType
ACT = ActivationFunctionType
B, L, S, N = 1792, 192, 48, 8
TR = 2 * L
U = 65536.0
BIG = 2.0 ** 26
CLS = (0, 4, 2, 6, 1, 5, 3, 7)
CFG = {"blocks": (((0, 96), (96, 48)), ((0, 96), (96, 96))),
       "nve": ((8, 8), (8, 8), (8, 8), (8, 8)), "nvs": ((8, 6), (4, 6), (6, 4), (6, 2)),
       "gv": ((0.33, 0.33), (0.125, 0.33), (0.25, 0.25), (0.0, 0.33)), "sub": (0.5, 0.5, 0, 0.5),
       "cS": (2, 2, 2, 2), "late": (0, 1), "mg": (1, 1, 0, 1), "neng": 8,
       "bx": (0, 2, 1, 0), "rep": (4, 2), "one": (2, 2, 5, 4), "con": 1276,
       "onV": (0, 0, 0, 0), "spl": (0, 2, 0, 0), "pw": (0, 1, 1, 1),
       "look": 60.0, "alpha": 20.0, "lat": 170.0, "lats": 210.0, "latp": 30.0, "latS": 60.0, "cyc": 0.83, "pe": 0.33,
       "g": 1.3, "sc": 2.8, "vfix": 12.0, "mn": 25, "vr": 0.7, "sfix": 200.0, "ldx": 3700.0, "hop": 3000.0}
DT = {"f": "float32", "b": "bfloat16", "i": "int32", "u": "uint16", "h": "float16"}


def col(a, c0, c1, step=1):
    return (a[0], a[1], a[2], a[3] + c0, a[3] + c1, step)


def rows(a, p0, p1):
    return (a[0], p0, p1) + a[3:]


def width(a):
    if a[0] == "ind":
        return 16 * width(a[2])
    return (a[4] - a[3] + a[5] - 1) // a[5]


def ind(win, off):
    return ("ind", win, off)


def cost(o, cfg):
    kind, n = o["shape"]
    cyc = cfg["cyc"]
    if kind == "fix":
        return n
    if kind == "pe":
        return n * cfg["pe"]
    if kind == "g":
        return 130 + 2 * n * cyc
    if kind == "gather":
        return (50 if o["eng"] == "V" else 65) + cfg["g"] * n * cyc
    if kind == "scatter":
        return 50 + cfg["sc"] * n * cyc
    if o["kind"] == "tt" and "ps" in (o["args"][1][0][:2], o["args"][2][0][:2]):
        n = n * cfg["vr"]
    return cfg["vfix" if o["eng"] == "V" else "sfix"] + max(cfg["mn"], n) * cyc


def build(cfg):
    ops = []
    top = {"f": 0, "b": 0, "i": 0, "u": 0, "h": 0}

    def new(k, n):
        a = top[k]
        top[k] = a + (n + 15) // 16 * 16
        return ("a" + k, 0, 128, a, a + n, 1)

    def bank(i, n, p=128):
        return ("ps%d" % i, 0, p, 0, n, 1)

    def flat(xs):
        r = []
        for a in xs:
            if isinstance(a, tuple):
                r += [a[1], a[2]] if a[0] == "ind" else [a]
        return r

    def add(eng, kind, args, out, ins, shape, **kw):
        rd = flat(ins)
        wr = [out]
        if out[0] == "ind":
            wr = [out[1]]
            rd = rd + [out[2]]
        o = {"eng": eng, "kind": kind, "args": args, "rd": rd, "wr": wr, "shape": shape, "n": len(ops), "after": []}
        o.update(kw)
        ops.append(o)
        return o

    def two(a):
        return a[0] in ("ab", "au", "ah", "xt", "sb0", "sb1")

    def shape(out, a, rate):
        n = width(out)
        if out[0] == "ind":
            return ("scatter", n)
        if a[0] == "ind":
            return ("gather", n)
        return ("flat", rate * n)

    def cp(out, a):
        return add("V", "cp", (out, a), out, [a], shape(out, a, 0.5 if two(out) and two(a) else 1))

    def tt(out, a, b, op):
        return add("V", "tt", (out, a, b, op), out, [a, b], shape(out, a, 1 if a[0][:2] == "ps" or b[0][:2] == "ps" else 2))

    def ts(out, a, s1, op0, s2=None, op1=None):
        return add("V", "ts", (out, a, s1, s2, op0, op1), out, [a, s1, s2], shape(out, a, 0.5 if two(out) and two(a) else 1))

    def ms(out, v):
        return add("V", "ms", (out, v), out, [], shape(out, out, 0.5 if two(out) else 1))

    def scan(out, d0, d1, init, op0, op1):
        return add("V", "scan", (out, d0, d1, init, op0, op1), out, [d0, d1], shape(out, d0, 1))

    def act(out, a, f=ACT.Identity, bias=0.0, scale=1.0):
        return add("S", "act", (out, a, f, bias, scale), out, [a], shape(out, a, 1))

    def mm(out, lhs, rhs, grp=None):
        c = max(min(64, width(lhs)), width(rhs)) * (4 if lhs[0] == "af" else 1)
        o = add("P", "mm", (out, lhs, rhs), out, [lhs, rhs], ("pe", c), grp=grp)
        if grp is not None:
            grp.append(o)
        return o

    def chain(terms):
        gp = []
        for t in terms:
            mm(*t, gp)["after"] += gp[-2:-1]

    def iota(out, pat, base=0, cm=0):
        return add("G", "iota", (out, pat, base, cm), out, [], ("g", width(out)))

    def dma(eng, out, a, dur, sem):
        return add(eng, "dma", (out, a), out, [a], ("fix", 60.0), dur=dur, sem=sem)

    XT = ("xt", 0, 128, 0, TR + B + 64, 1)
    CT = ("ct", 0, 128, 0, TR + B + S, 1)
    dr = lambda nm, a, b: (nm, 0, 128, a, b, 1)

    eni, joi = new("i", 24), new("i", 18)
    dma("S", eni, dr("en", 0, 24), 2000.0, "ld0")
    dma("S", joi, dr("jo", 0, 18), 2000.0, "ld2")
    o = dma("Y", col(XT, TR, TR + B), dr("x", 0, B), 1500 + (cfg["ldx"] - 1500) / 3, "ld3")
    dma("Y", col(CT, TR, TR + B), dr("ch", 0, B), cfg["ldx"], "ld1")["behind"] = o
    ms(col(XT, TR, TR + 1), 31.0)

    pi, t_i = new("i", 1), new("i", 2)
    idt, ids = new("f", 256), new("f", TR + B + S)
    JB, JR, G18 = new("f", 128), new("f", L), new("f", 144)
    iota(pi, [[0, 1]], 0, 1)
    iota(idt, [[1, 256]])
    iota(JB, [[1, 8], [0, 16]])
    iota(JR, [[0, 12], [1, 16]])
    iota(G18, [[1, 8], [0, 18]])
    G40 = new("f", 40)
    iota(G40, [[0, 5], [1, 8]])
    if cfg["con"] >> 10 & 1:
        iota(col(CT, 0, TR), [[0, TR]])
    else:
        ms(col(CT, 0, TR), 0)
    ms(col(CT, TR + B, TR + B + S), 0)
    ms(col(XT, 0, TR), 0.0)

    def fill(out, v):
        return act(out, col(idt, 0, width(out)), ACT.Identity, v, 0.0)

    def scale(k, out, a, v):
        return act(out, a, ACT.Identity, 0.0, v) if cfg["con"] >> k & 1 else ts(out, a, v, ALU.mult)

    def const(k, out, v):
        return fill(out, v) if cfg["con"] >> k & 1 else ms(out, v)

    act(col(ids, 0, 256), idt, ACT.Identity, -4096.0)
    ts(col(ids, 256, 512), idt, 256 - 4096.0, ALU.add)
    for a, b, on_s in ((512, 1024, 1), (1024, 1536, 0), (1536, 2048, 1), (2048, TR + B + S, 0)):
        if on_s:
            act(col(ids, a, b), col(ids, 0, b - a), ACT.Identity, float(a))
        else:
            ts(col(ids, a, b), col(ids, 0, b - a), float(a), ALU.add)

    cols = new("f", 8)
    pc, gcol, rc, r23, p18 = [col(cols, j, j + 1) for j in range(5)]
    cp(pc, pi)
    ts(col(t_i, 0, 1), pi, 4, ALU.arith_shift_right)
    ts(col(t_i, 1, 2), pi, 15, ALU.bitwise_and)
    cp(col(cols, 1, 3), t_i)
    ts(r23, rc, -1.0, ALU.mult, 23.0, ALU.add)
    ts(p18, gcol, 2.0, ALU.mult, pc, ALU.add)
    I, NI, I8, BO, NBO, TRI, t1 = [new("b", 128) for _ in range(7)]
    IH, M16, OFF = new("h", 128), new("f", L), new("b", L)
    ts(I, col(idt, 0, 128), pc, ALU.is_equal)
    scale(0, NI, I, -1.0)
    scale(1, I8, I, -8192.0)
    cp(IH, I)
    ts(BO, JB, gcol, ALU.is_equal, U, ALU.mult)
    scale(2, NBO, BO, -1.0)
    ts(M16, JR, rc, ALU.is_equal)
    act(OFF, M16, ACT.Identity, -2.0 ** 20, 5 * 2.0 ** 18)
    add("G", "sel", (t1, BO, [[1, 128]], ALU.is_gt, 0.0, 0, -1), t1, [BO], ("g", 148))
    add("G", "sel", (TRI, t1, [[1, 128]], ALU.not_equal, -512 * U, 0, -1), TRI, [t1], ("g", 148))
    B8f, RH, B16, B8 = new("f", 8), new("f", 40), new("f", 8), {}
    ts(B8f, col(idt, 0, 8), gcol, ALU.is_equal)
    ts(RH, G40, gcol, ALU.is_equal, col(B8f, 7, 8), ALU.max)
    ts(col(RH, 16, 32), col(RH, 16, 32), -1.0, ALU.mult)
    for v in (1, -1, 2, -2):
        B8[v] = new("b", 8)
        ts(B8[v], B8f, v * U, ALU.mult)
    if 2 in cfg["cS"]:
        IF = new("f", 128)
        act(IF, I)
        ts(B16, B8f, 1.0 / 16, ALU.mult)
    PAY, P0 = new("h", 144), new("h", 144)
    CK, BX = new("b", 144), new("b", 144)
    ts(PAY, col(idt, 0, 144), p18, ALU.is_equal)
    ts(BX, G18, gcol, ALU.is_equal, U, ALU.mult)
    ms(CK, 0.0)
    if min(cfg["cS"]) < 2:
        cp(P0, CK)
    for c in (16, 17):
        ms(col(BX, c, 144, 18), 0.0)
        if min(cfg["cS"]) < 2:
            ts(col(P0, c, 144, 18), B8f, 1.0 / 16, ALU.mult)
    for c in (16, 17):
        ms(col(CK, c, 144, 18), -250 * U)
    RK = [new("f", 144), new("f", 128)]
    const(3, RK[0], 2048.0)
    ms(col(RK[0], 0, 144, 18), -2.0 ** 40)
    ms(col(RK[0], 16, 144, 18), 16384 - 251 * U)
    ms(col(RK[0], 17, 144, 18), 0.0)
    const(4, RK[1], 4096.0)
    ms(col(RK[1], 0, 128, 16), -2.0 ** 40)
    xoff = [new("u", 8), new("u", 8)]
    ts(xoff[0], col(idt, 0, 8), 18.0, ALU.mult, 17.0, ALU.add)
    ts(xoff[1], col(idt, 0, 8), 16.0, ALU.mult, 15.0, ALU.add)
    CR = new("b", 24)
    for j, v in enumerate((1.5 * 2.0 ** 34, 1.5 * 2.0 ** 39, 1.5 * 2.0 ** 35)):
        ms(col(CR, 8 * j, 8 * j + 8), v)
    lanew, blank, tr2 = new("f", 12), new("f", 12), new("f", 12)
    ts(lanew, col(idt, 0, L, 16), rc, ALU.add)
    ts(blank, lanew, float(L), ALU.add)
    ts(tr2, lanew, L - 512.0, ALU.add, U, ALU.mult)
    E, c160, ONE = new("b", 32), new("b", L), new("b", 12)
    ts(E, col(idt, 0, 32), r23, ALU.is_equal, 4096.0, ALU.mult)
    if 0 in cfg["bx"]:
        const(5, c160, -160.0)
    ms(ONE, 1.0)
    SB = [("sb%d" % t, 0, 128, 0, 2 * L + 16, 1) for t in range(2)]
    for t in range(2):
        ms(col(SB[t], 0, 64), 0.0)
    SC = [[new("f", w) for q in range(2)] for w in (144, 128)]
    for k in range(2):
        for q in range(2):
            if cfg["con"] >> (8 + k) & 1:
                iota(SC[k][q], [[0, width(SC[k][q])]], -5 * 65536 - 16384 - 1023)
            else:
                const(6 + k, SC[k][q], -5 * U - 16384 - 1023)
    nend = new("u", 24)
    ms(col(nend, 8, 12), TR)

    KX = [new("b", 16 * L) for _ in range(3)]
    EL = [[new("b", 16 * 96) for _ in range(2)] for _ in range(2)]
    EQ = [new("b", 1248) for _ in range(2)]
    AX = [new("f", 128) for _ in range(2)]
    KB, XB, DB, M0, M1 = (0, 1), (2, 3), (4, 5), 6, 7
    dnext = [0]
    LB = ("lb", 0, 128, 0, S, 1)

    def distances(q, m, kx, xr, sg, nv, key, grp, rep, cut=0, spl=0):
        def units(cs, r):
            us = []
            for c in cs:
                if r == 4 and c >= 4 and c - 4 in cs:
                    continue
                us += [(c, 4)] if r == 4 and c + 4 in cs else [(c, 8)] if r > 1 else [(c, 16), (c + 8, 16)]
            return us
        W = width(key)
        slot = lambda s: col(key, s, W, W // 8)
        parts = ((0, spl), (spl, m)) if spl else ((0, m),)
        sums = {(s, p0): mm(rows(slot(s), p0, p1), col(kx, 16 * p0 + s, 16 * p1, 16), B8[sg], grp)
                for s in range(16) if s % 8 in CLS[:nv] for p0, p1 in parts}
        vs, ss = units(CLS[:nv], rep), units(CLS[nv:], 4)
        xps, at, el = {}, 0, EL[q][sg < 0]
        for r in sorted(set(16 // st for c, st in vs)):
            xps[r] = col(bank(XB[q], 512), at, at + r * m)
            at += r * m
            for j in range(r):
                mm(col(xps[r], j, r * m, r), I, xr)
        mins, at = [], 0
        todo = sorted([(k / len(vs), 0, u) for k, u in enumerate(vs)] + [(k / len(ss), 1, u) for k, u in enumerate(ss)])
        for _, on_s, (c, st) in todo:
            r = 16 // st
            e = col(el, at, at + r * m)
            at += r * m
            if on_s:
                d = bank(DB[dnext[0] % 2], r * m)
                dnext[0] += 1
                dg = []
                mm(d, I, col(kx, c, 16 * m, st), dg)
                for j in range(r):
                    mm(col(d, j, r * m, r), NI, xr, dg)
                act(e, d, ACT.Abs)
            else:
                for a, b in ((0, cut), (cut, m)):
                    if b > a:
                        tt(col(e, r * a, r * b), col(kx, 16 * a + c, 16 * b, st), col(xps[r], r * a, r * b), ALU.min)
            for j in range(r):
                for p0, p1 in ((0, m),) if on_s else parts:
                    o = mm(rows(slot(c + st * j), p0, p1), col(e, r * p0 + j, r * p1, r), B8[sg if on_s else -2 * sg], grp)
                    if not on_s:
                        o["after"].append(sums[c + st * j, p0])
                        mins.append(o)
        at = 0
        for n in (8, 4, 2, 1):
            if nv & n:
                if sg < 0 or n >= 4:
                    mm(col(key, CLS[at], W, 8 // n), xr, col(BX if sg > 0 else NBO, CLS[at], W, 8 // n), grp)["after"] += mins
                else:
                    for s in range(CLS[at], 16, 8 // n):
                        mm(slot(s), xr, B8[1], grp)["after"] += mins
                at += n

    def best(k, q, m, key):
        scan(rows(SC[k][q], 0, m), rows(RK[k], 0, m), key, 0.0, ALU.add, ALU.max)
        tt(AX[q], ind(SC[k][q], xoff[k]), col(M16, 0, 128), ALU.mult)

    def waits(bk, nu, nf, nb, buf):
        Lr, at, pd, gp = 16 * nb, 0, bank(bk, 16 * nb), []
        nrep, xw = new("u", Lr), new("b", Lr)
        ts(nrep, ind(ids, col(nu, 0, nb)), 4096.0, ALU.add)
        mm(pd, I, col(OFF, 0, Lr), gp)
        for b in range(nb):
            e = col(buf, at, at + Lr - 16 * b)
            at += Lr - 16 * b
            ts(e, col(nrep, 16 * b, Lr), col(nf, b, b + 1), ALU.is_equal, 512 / U, ALU.mult)
            mm(col(pd, 16 * b, 16 * b + 16), TRI, col(e, 0, 16), gp)
            if b + 1 < nb:
                mm(col(pd, 16 * b + 16, Lr), BO, col(e, 16, Lr - 16 * b), gp)
        ts(xw, pd, 500.0, ALU.min, 0.0, ALU.max)
        return xw

    nu0, nf0, cu0 = new("u", 24), new("f", 24), new("u", 24)
    ts(nu0, eni, float(TR), ALU.add)
    ts(nf0, eni, float(TR), ALU.add)
    first = [waits(DB[t], col(nu0, 12 * t, 12 * t + 12), col(nf0, 12 * t, 12 * t + 12), 9 + 3 * t, EQ[t]) for t in range(2)]
    st = {}
    late = {}
    for rnd in range(2):
        Lr = L - S if rnd == 0 else L
        nb = Lr // 16
        NW = B if rnd == 0 else B + S
        al = lambda a: col(a, 0, nb)
        nu, nf, cu = [col(a, 12 * rnd, 12 * rnd + 12) for a in (nu0, nf0, cu0)]
        cp(col(cu, 0, 9), col(joi, 9 * rnd, 9 * rnd + 9))
        z0 = nf
        if rnd == 1:
            ts(col(cu, 9, 12), col(lanew, 0, 3), float(B), ALU.add)
            cnt = col(XT, TR + B + S, TR + B + S + 1)
            lone, z0, zt, idle = new("f", 3), new("f", 12), new("f", 3), new("b", S)
            cp(col(z0, 0, 9), col(nf, 0, 9))
            ts(lone, col(lanew, 0, 3), cnt, ALU.is_lt)
            tt(zt, col(nf, 9, 12), lone, ALU.mult)
            ts(col(z0, 9, 12), zt, float(TR), ALU.max)
            k1, kd = new("f", S), new("f", S)
            ts(k1, col(idt, 0, S), 1.0, ALU.add)
            tt(kd, k1, col(M16, 0, S), ALU.mult)
            ts(idle, kd, cnt, ALU.is_gt, 500.0, ALU.mult)
        for step in range(2):
            si = 2 * rnd + step
            guests = si == 2
            nw1 = B if step == 0 else NW
            xw1, xw = col(XT, TR, TR + nw1), col(XT, TR, TR + NW)
            ku, kf = new("u", Lr), new("h", Lr)
            xn, xc, xo, ad, bl, mask = [new("b", Lr) for _ in range(6)]
            ou, su, wu = new("u", 12), new("u", 12), new("u", 12)
            th, put, stay, keep, a1, a2, a3, a4, nf2 = [new("f", 12) for _ in range(9)]
            wipe, held = new("b", 12), new("h", 12)
            nu2 = new("u", 12) if step == 0 else col(nend, 12 * rnd, 12 * rnd + 12)
            cm, nl = new("f", Lr), new("i", Lr)
            kxs = KX[(0, 1, 0, 2)[si]]
            ch = [(q, l0, m, l0 // 16, (l0 + m) // 16) for q, (l0, m) in enumerate(cfg["blocks"][rnd])]
            take = lambda bit, out, a, si=si: (cp if cfg["onV"][si] & bit else act)(out, a)
            spl = [(32 if m <= 64 else 64) if cfg["spl"][si] >> q & 1 else 0 for q, l0, m, b0, b1 in ch]
            cuts = [spl[q] or int(m * cfg["sub"][si]) // 2 * 2 for q, l0, m, b0, b1 in ch]
            one = cfg["one"][si]
            for q, l0, m, b0, b1 in ch:
                ln = lambda a: col(a, l0, l0 + m)
                wr = lambda a: col(a, b0, b1)
                if not one & 1:
                    cp(ln(ku), ind(col(CT, 0, TR + nw1), wr(nu)))
                elif q == 0:
                    cp(ku, ind(col(CT, 0, TR + nw1), al(nu)))
                if not one & 2:
                    take(2, ln(xn), ind(col(XT, 0, TR + nw1), wr(nu)))
                elif q == 0:
                    take(2, xn, ind(col(XT, 0, TR + nw1), al(nu)))
                mv = int(round(m * cfg["gv"][si][q] / 2)) * 2
                cut = cuts[q]
                for a, b in zip(sorted({0, mv, cut}), sorted({mv, cut, m} - {0})):
                    if b > a:
                        (cp if b <= mv else act)(col(kxs, 16 * (l0 + a), 16 * (l0 + b)), ind(xw1, col(ku, l0 + a, l0 + b)))
                if not one & 4:
                    cp(ln(kf), ln(ku))
            if one & 4:
                cp(kf, ku)
            if cfg["cS"][si] == 2:
                crep = new("f", Lr)
                act(crep, ind(ids, al(cu)), ACT.Identity, 4096.0)
            else:
                crep = new("h", Lr)
                ts(crep, ind(ids, al(cu)), 4096.0, ALU.add)
            if guests:
                take(4, col(xc, 0, L - S), ind(xw1, col(cu, 0, 9)))
            else:
                take(4, xc, ind(xw, al(cu)))
            if cfg["bx"][si]:
                x160 = new("b", Lr)
                if cfg["bx"][si] == 1:
                    ts(x160, xn, -160.0, ALU.add)
                else:
                    act(x160, xn, ACT.Identity, -160.0)
            else:
                x160 = col(c160, 0, Lr)
            xwt = first[rnd] if step == 0 else waits(M1, nu, nf, nb, EQ[0])

            def blends(l0, m):
                ln = lambda a: col(a, l0, l0 + m)
                pm = bank(M0, 2 * m)
                own = min(m, L - S - l0) if guests else m
                for c0, sgn in ((0, NI), (m, I))[:1 if cfg["bx"][si] else 2]:
                    gp = []
                    mm(col(pm, c0, c0 + m), sgn, ln(xn), gp)
                    mm(col(pm, c0, c0 + own), I, col(xc, l0, l0 + own), gp)
                    if own < m:
                        mm(col(pm, c0 + own, c0 + m), I, col(XT, TR + B, TR + B + S), gp)
                act(ln(ad), col(pm, 0, m), ACT.Abs)
                c0 = 0 if cfg["bx"][si] else m
                act(ln(bl), col(pm, c0, c0 + m), ACT.Identity, 159.75, 0.5)

            def worst(q, l0, m, b0, b1):
                ln = lambda a: col(a, l0, l0 + m)
                wr = lambda a: col(a, b0, b1)
                key, grp = bank(KB[q], 144, m), []
                mm(key, col(I, 0, m), CK, grp)
                mm(key, ln(kf), PAY, grp)
                if cfg["cS"][si] == 2:
                    mm(col(key, 16, 144, 18), ln(crep), B16, grp)
                    mm(col(key, 17, 144, 18), ln(crep), B16, grp)
                else:
                    mm(key, ln(crep), P0, grp)
                mm(col(key, 16, 144, 18), ln(ad), B8[1], grp)
                mm(col(key, 17, 144, 18), ln(xw_[q]), B8[1], grp)
                distances(q, m, col(kxs, 16 * l0, 16 * (l0 + m)), ln(xn), 1, cfg["nve"][si][q], key, grp, cfg["rep"][0],
                          cuts[q], spl[q])
                best(0, q, m, key)
                w = bank(XB[q], 24)
                chain([(w, AX[q], col(RH, 16, 40)), (col(w, 0, 16), I, col(CR, 0, 16)), (col(w, 0, 16), NI, col(CR, 0, 16)),
                       (col(w, 0, 16), AX[q], col(RH, 0, 16)), (col(w, 8, 16), I, col(CR, 0, 8)), (col(w, 8, 16), NI, col(CR, 0, 8))])
                k = b1 - b0
                ts(wr(ou), col(w, 0, k), 1023.0, ALU.add)
                ts(wr(su), col(w, 8, 8 + k), 1.0 / 2048, ALU.mult, 8.0, ALU.add)
                ts(wr(put), col(w, 8, 8 + k), 0.0, ALU.is_ge, 4096.0, ALU.mult)
                ts(wr(stay), col(w, 16, 16 + k), -U / 2, ALU.is_ge)
                ts(wr(wipe), col(w, 16, 16 + k), -U / 2, ALU.is_ge, 2.0 ** 36, ALU.mult)
                ts(wr(th), col(w, 16, 16 + k), 242 * U, ALU.is_ge, BIG, ALU.mult)
                take(1, ln(xo), ind(xw1 if guests and l0 + m <= L - S else xw, wr(ou)))

            def marks(l0, m):
                b0, b1 = l0 // 16, (l0 + m) // 16
                wr = lambda a: col(a, b0, b1)
                take(8, col(mask, l0, l0 + m), ind(E, wr(su)))
                if step == 0:
                    if guests and b1 == nb:
                        tt(col(th, 9, 12), col(th, 9, 12), lone, ALU.mult)
                    tt(wr(a1), wr(nf), wr(th), ALU.min)
                    tt(wr(keep), wr(a1), wr(blank), ALU.max)
                    ts(wr(a4), wr(keep), -float(TR), ALU.add)
                tt(wr(held), wr(a4), wr(stay), ALU.mult)

            def nearest(q, l0, m, b0, b1, si=si, step=step, kxs=kxs, kf=kf, xo=xo, mask=mask, wipe=wipe, held=held,
                        nu2=nu2, nf2=nf2):
                ln = lambda a: col(a, l0, l0 + m)
                wr = lambda a: col(a, b0, b1)
                key, grp = bank(KB[q], 128, m), []
                mm(key, ln(kf), IH, grp)
                distances(q, m, col(kxs, 16 * l0, 16 * (l0 + m)), ln(xo), -1, cfg["nvs"][si][q], key, grp, cfg["rep"][1])
                mm(key, ln(mask), I8, grp)
                best(1, q, m, key)
                k = b1 - b0
                w, ax, c = bank(XB[q], k), rows(AX[q], 0, m), col(CR, 16, 16 + k)
                chain([(w, ax, rows(col(RH, 16, 16 + k), 0, m)), (w, I, c), (w, NI, c), (w, ax, rows(col(RH, 0, k), 0, m)),
                       (w, I, wr(wipe)), (w, NI, wr(wipe)), (w, IH, wr(held))])
                ts(wr(nu2), w, float(TR), ALU.add)
                if step == 0:
                    ts(wr(nf2), w, float(TR), ALU.add)

            if step == 1:
                dd = new("f", 12)
                ts(al(dd), al(nf), float(TR), ALU.is_lt, BIG, ALU.mult)
                tt(al(a1), al(z0), al(dd), ALU.min)
                tt(al(keep), al(a1), al(nf), ALU.max)
                ts(al(a4), al(keep), -float(TR), ALU.add)
            xw_ = [xwt, xwt]
            if guests:
                xw_[1] = new("b", Lr)
                cp(col(xw_[1], 96, L - S), col(xwt, 96, L - S))
                tt(col(xw_[1], L - S, L), col(xwt, L - S, L), idle, ALU.max)
            else:
                blends(0, Lr)
            for c in ch:
                if guests:
                    if c[0] == 1:
                        for k in range(2):
                            if cfg["late"][k] == 1:
                                late[k][0](*late[k][1])
                    blends(c[1], c[2])
                worst(*c)
                if not cfg["mg"][si]:
                    marks(c[1], c[2])
            if cfg["mg"][si]:
                marks(0, Lr)
            if cfg["pw"][si]:
                for a in range(nb):
                    ts(col(wu, a, a + 1), col(put, a, a + 1), col(nf, a, a + 1), ALU.min, col(lanew, a, a + 1), ALU.max)
            else:
                tt(al(a3), al(nf), al(put), ALU.min)
                tt(al(a2), al(a3), al(lanew), ALU.max)
                cp(al(wu), al(a2))
            tt(ind(col(XT, 0, TR + NW), al(wu)), bl, x160, ALU.add)
            if step == 1:
                live, inc, xs_, b1_, pu = new("b", 12), new("b", 12), new("b", Lr), new("f", 12), new("u", 12)
                tt(al(live), al(stay), al(th), ALU.is_le)
                scan(al(inc), al(ONE), al(live), 0.0, ALU.mult, ALU.add)
                pp, gp = bank(M1, 16), []
                mm(col(pp, 0, nb), TRI, al(live), gp)
                mm(col(pp, 1, nb), BO, col(inc, 0, nb - 1), gp)
                if rnd == 0:
                    mm(col(pp, 12, 13), BO, col(inc, nb - 1, nb))
                tt(al(b1_), col(pp, 0, nb), al(tr2), ALU.min)
                if rnd == 0:
                    b2_, b3_ = new("f", 12), new("f", 12)
                    ts(col(SB[0], S, S + 1), col(pp, 12, 13), 1.0 / U, ALU.mult)
                    ts(al(b2_), al(b1_), (S - 512) * U, ALU.is_ge, 16 * U, ALU.mult)
                    tt(al(b3_), al(b1_), al(b2_), ALU.add)
                    b1_ = b3_
                ts(al(pu), al(b1_), 1.0 / U, ALU.mult, 512.0, ALU.add)
                take(16, xs_, ind(xw, al(ou)))
                cp(ind(SB[rnd], al(pu)), xs_)
                w = 64 if rnd == 0 else S
                tok = ("tok%d" % rnd, 0, 128, 0, 1, 1)
                st["send%d" % rnd] = add("G", "send", (rnd, col(SB[rnd], 0, w)), tok, [col(SB[rnd], 0, w)], ("fix", 300.0),
                                         dur=1500.0, sem="snt%d" % rnd)
            pa, ga_ = bank(M1, Lr), []
            if cfg["cS"][si]:
                pb, gb_ = bank(M0, Lr), []
                mm(pb, IF if cfg["cS"][si] == 2 else IH, crep, gb_)
                mm(pb, I, mask, gb_)
                act(cm, pb, ACT.Identity, -4096.0)
            else:
                tt(cm, ind(ids, al(cu)), mask, ALU.add)
            mm(pa, IH, kf, ga_)
            mm(pa, NI, mask, ga_)
            tt(nl, pa, cm, ALU.max)
            cp(ind(col(CT, 0, TR + NW), al(wu)), nl)
            if si == 3:
                for k in range(2):
                    if cfg["late"][k] == 2:
                        late[k][0](*late[k][1])
            for c in ch:
                if si == 1 and cfg["late"][c[0]]:
                    late[c[0]] = (nearest, c)
                else:
                    nearest(*c)
            if si == 3:
                for k in range(2):
                    if cfg["late"][k] == 3:
                        late[k][0](*late[k][1])
            if step == 1:
                land = col(XT, TR + B, TR + B + 64) if rnd == 0 else LB
                o = add("X", "arrive", (rnd,), land, [], ("fix", 0.0), dur=cfg["hop"], sem="arr%d" % rnd)
                o["soft"] = st["send%d" % rnd]
            nu, nf, cu = nu2, nf2, ou
    yf = new("f", 2 * L)
    ms(col(XT, TR, TR + 1), 0.0)
    o = dma("Y", dr("yx", 0, B + S), col(XT, TR, TR + B + S), 3000.0, "st0")
    o["after"].append(st["send1"])
    dma("Y", dr("yx", B + S, B + 2 * S), LB, 2000.0, "st1")
    for t in range(2):
        cp(col(yf, t * L, t * L + L), ind(CT, col(nend, 12 * t, 12 * t + 12)))
        dma("S", dr("yl", t * L, t * L + L), col(yf, t * L, t * L + L), 2000.0, "st%d" % (2 + t))
    return ops, top


def link(ops):
    seen = {}
    for o in ops:
        deps, order = set(), set()
        acc = [(a, False) for a in o["rd"]] + [(a, True) for a in o["wr"]]
        for a, w in acc:
            ps = a[0][:2] == "ps"
            for (p, b, pw) in seen.get(a[0], ()):
                if ps and p["eng"] != o["eng"]:
                    deps.add(p["n"])
                elif ps and o["eng"] == "P":
                    if o["grp"] is None or p["grp"] is not o["grp"] or o["grp"][0] is p:
                        order.add(p["n"])
                elif (w or pw) and a[3] < b[4] and b[3] < a[4]:
                    deps.add(p["n"])
        for a, w in acc:
            seen.setdefault(a[0], []).append((o, a, w))
        for p in o["after"]:
            (order if p["eng"] == "P" and o["eng"] == "P" else deps).add(p["n"])
        if "behind" in o:
            order.add(o["behind"]["n"])
        if o["kind"] == "arrive":
            deps = set()
        o["deps"], o["order"] = deps, order - deps


def schedule(ops, cfg):
    n = len(ops)
    more = {"P": cfg["latp"], "S": cfg["latS"]}
    lat = lambda p, o: cfg["lats" if p["eng"] == o["eng"] else "lat"] + more.get(p["eng"], 0)
    pre = [[(d, lat(ops[d], o)) for d in o["deps"]] + [(d, -ops[d].get("dur", 0.0)) for d in o["order"]] for o in ops]
    for o in ops:
        o["cost"] = cost(o, cfg)
        if "soft" in o:
            pre[o["n"]].append((o["soft"]["n"], 0.0))
    suc = [[] for _ in ops]
    for i in range(n):
        for d, l in pre[i]:
            suc[d].append((i, l))
    span = [o["cost"] + o.get("dur", 0.0) for o in ops]
    prio = [0.0] * n
    for i in range(n - 1, -1, -1):
        prio[i] = span[i] + max([prio[j] + l for j, l in suc[i]] + [0.0])
    left = [len(p) for p in pre]
    rdy, free, queues, end = [0.0] * n, {}, {}, 0.0
    pool = [i for i in range(n) if left[i] == 0]
    while pool:
        t0, e0 = min((max(rdy[i], free.get(ops[i]["eng"], 0.0)), ops[i]["eng"]) for i in pool)
        cand = [i for i in pool if ops[i]["eng"] == e0 and rdy[i] <= t0 + cfg["look"]]
        i = max(cand, key=lambda j: (prio[j] - cfg["alpha"] * max(0.0, rdy[j] - t0), -j))
        pool.remove(i)
        o = ops[i]
        o["t"] = max(t0, rdy[i])
        free[e0] = o["t"] + o["cost"]
        queues.setdefault(e0, []).append(o)
        fin = o["t"] + span[i]
        end = max(end, fin)
        for j, l in suc[i]:
            rdy[j] = max(rdy[j], fin + l)
            left[j] -= 1
            if left[j] == 0:
                pool.append(j)
    return queues, end


def plan(cfg):
    ops, top = build(cfg)
    link(ops)
    queues, end = schedule(ops, cfg)
    pos = {}
    for e, qu in queues.items():
        for k, o in enumerate(qu):
            pos[o["n"]] = k
    for e, qu in queues.items():
        got = {}
        for o in qu:
            need = {}
            for d in o["deps"]:
                p = ops[d]
                k = p.get("sem") or p["eng"]
                if pos[d] > got.get(k, -1) and pos[d] > need.get(k, (-1, None))[0]:
                    need[k] = (pos[d], p)
            o["waits"] = [v[1] for v in need.values()]
            for k, v in need.items():
                got[k] = v[0]
                v[1]["sig"] = True
    total = {}
    for e, qu in queues.items():
        c = 0
        for o in qu:
            if "sem" not in o and o.get("sig"):
                c += 1
                o["cnt"] = c
        total[e] = c
    for o in queues["P"]:
        gr = o["grp"]
        o["start"] = gr is None or gr[0] is o
        o["stop"] = gr is None or max(pos[p["n"]] for p in gr) == pos[o["n"]]
    return ops, top, queues, total, end


PLAN = plan(CFG)
SCRATCH = {"xt": ("sbuf", [128, TR + B + 64], "bfloat16"), "ct": ("sbuf", [128, TR + B + S], "int32"),
           "sb0": ("sbuf", [128, 2 * L + 16], "bfloat16"), "sb1": ("sbuf", [128, 2 * L + 16], "bfloat16"),
           "lb": ("dram", [128, S], "bfloat16"),
           "rb0": ("sbuf", [128, 64], "bfloat16"), "rb1": ("dram", [128, S], "bfloat16")}
for _k in "fbiuh":
    SCRATCH["a" + _k] = ("sbuf", [128, PLAN[1][_k]], DT[_k])
for _k in range(8):
    SCRATCH["ps%d" % _k] = ("psum", [128, 512], "float32")
SEMAPHORES = ["cV", "cS", "cP", "cG", "ld0", "ld1", "ld2", "ld3", "st0", "st1", "st2", "st3",
              "snt0", "snt1", "arr0", "arr1", "rin0", "rin1", "rout"]


def relay_of(core, cores, topo):
    r = cores.index(core)
    dsts = [cores[(r + 1 + t) % N] for t in range(2)]
    ok = [c for c in topo.cores_of(core) if c not in cores and all(topo.may_write(c, d) for d in dsts)]
    near = [c for c in ok if topo.die(c) == topo.die(core)]
    return near[0]


def some(engines, k):
    m = 0
    for e in engines[:k]:
        m |= 1 << e
    return m


def rank_program(g, core, T, topo):
    cores = list(T.cores)
    ne = CFG["neng"]
    ops, top, queues, total, end = PLAN

    def ap(a):
        if not isinstance(a, tuple):
            return a
        if a[0] == "ind":
            return ap(a[1]).indirect(ap(a[2]))
        if a[5] == 1:
            return T[a[0]][a[1]:a[2], a[3]:a[4]]
        return T[a[0]][a[1]:a[2], a[3]:a[4]:a[5]]

    rank = T.rank_of(core)
    if rank is None:
        for r, c in enumerate(cores):
            if relay_of(c, cores, topo) == core:
                far = cores[(r + 2) % N]
                for t in range(2):
                    d = cores[(r + 1 + t) % N]
                    rid, pid = topo.addr(d, core)
                    eng = [e for e in topo.engines(core, d) if e in topo.engines(core, far)]
                    land = T.xt[:, TR + B:TR + B + 64] if t == 0 else T.lb[:]
                    g.wait_ge(T.sem["rin%d" % t], ne)
                    g.remote_dma(land, T["rb%d" % t][:], T.sem["arr%d" % t], T.sem.rout, pid, rid, some(eng, ne))
                g.wait_ge(T.sem.rout, 2 * ne)
        return

    relay = relay_of(core, cores, topo)
    eng = {"V": g.vector, "S": g.scalar, "P": g.tensor, "G": g, "Y": g.sync}
    for e in ("Y", "S", "G", "V", "P"):
        q = eng[e]
        for o in queues[e]:
            for p in o["waits"]:
                if "sem" in p:
                    q.wait_ge(T.sem[p["sem"]], 16 if p["kind"] == "dma" else ne)
                else:
                    q.wait_ge(T.sem["c" + p["eng"]], p["cnt"])
            k = o["kind"]
            a = [ap(v) for v in o["args"]]
            if k == "send":
                t = o["args"][0]
                rid, pid = topo.addr(relay, core)
                g.remote_dma(T["rb%d" % t][:], a[1], T.sem["rin%d" % t], T.sem["snt%d" % t], pid, rid,
                             some(topo.engines(core, relay)[::-1], ne))
                continue
            if k == "dma":
                q.dma_start(a[0], a[1]).then_inc(T.sem[o["sem"]], 16)
                continue
            if k == "cp":
                r = q.tensor_copy(a[0], a[1])
            elif k == "tt":
                r = q.tensor_tensor(a[0], a[1], a[2], a[3])
            elif k == "ts":
                r = q.tensor_scalar(a[0], a[1], a[2], a[3], a[4]) if a[5] is None else q.tensor_scalar(*a)
            elif k == "ms":
                r = q.memset(a[0], a[1])
            elif k == "scan":
                r = q.tensor_tensor_scan(*a)
            elif k == "act":
                r = q.activation(a[0], a[1], a[2], bias=a[3], scale=a[4])
            elif k == "mm":
                r = q.matmul(a[0], a[1], a[2], o["start"], o["stop"])
            elif k == "sel":
                r = q.affine_select(*a)
            elif o["args"][0][0] in ("ai", "ct"):
                r = q.iota(a[0], a[1], a[2], a[3])
            else:
                r = q.iota(a[0], a[1], a[2], a[3], allow_small_or_imprecise_dtypes=True)
            if o.get("sig"):
                r.then_inc(T.sem["c" + e], 1)
    g.wait_ge(T.sem.snt0, ne)
    for s in ("st0", "st1", "st2", "st3"):
        g.wait_ge(T.sem[s], 16)
